import numpy as np
import ml_dtypes


def mxq(x, axis, fmt="e4m3"):
    dtype, down = {"e4m3": (ml_dtypes.float8_e4m3fn, 7), "e5m2": (ml_dtypes.float8_e5m2, 14)}[fmt]
    v = np.moveaxis(np.asarray(x, np.float32).astype(ml_dtypes.bfloat16).astype(np.float64), axis, -1)
    blocks = v.reshape(v.shape[:-1] + (-1, 32))
    amax = np.abs(blocks).max(-1, keepdims=True)
    byte = np.maximum(np.where(amax > 0, np.frexp(amax)[1] - 1 + 127, 0) - down, 1)
    scale = np.exp2(byte - 127.0)
    codes = (blocks / scale).astype(np.float32).astype(dtype).astype(np.float64)
    return np.moveaxis((codes * scale).reshape(v.shape), -1, axis)


WIDE = False


def mx_kscale(k):
    if not WIDE:
        return np.ones(k)
    levels = np.array([10, -10, 5, -5, 0])
    if k % 512:
        return np.exp2(np.random.permutation(np.resize(levels, k // 32))).repeat(32)
    a = np.empty((k // 512, 16))
    for p in range(k // 512):
        a[p, :8] = np.random.permutation(np.resize(levels, 8))
        for g in range(8):
            far = levels[np.abs(levels - a[p, g]) >= 10]
            a[p, g + 8] = far[np.random.randint(len(far))]
    return np.exp2(a.ravel()).repeat(32)


def f64(x):
    return np.asarray(x).astype(np.float64)


def striped(idx):
    return np.tile(idx.reshape(-1, 16).T, (8, 1)).astype(np.uint16)


def unstriped(offs):
    return offs[:16].T.reshape(-1).astype(np.int64)


def relu2(v):
    return np.maximum(v, 0.0) ** 2


K, T, E, C, H, N = 1536, 1024, 6, 128, 512, 256


def by_expert(wq, xq):
    return np.concatenate([wq[e].T @ xq[:, e * C:(e + 1) * C] for e in range(E)], axis=1)


def setup_inputs():
    n = np.random.standard_normal
    s = mx_kscale(K)[:, None]
    u = mx_kscale(H)
    return {
        "xT": (n((K, T)) * s).astype(np.float32),
        "w1": (n((E, K, H)) / np.sqrt(K) / s[None] * u[None, None, :]).astype(np.float32),
        "w2": (n((E, H, N)) / np.sqrt(H) / u[None, :, None] ** 2).astype(np.float32),
        "gate": np.tile(np.random.uniform(0.2, 1.0, E * C), (N, 1)).astype(np.float32),
        "offs": striped(np.random.permutation(T)[:E * C]),
        "dst": striped(np.random.permutation(T)[:E * C]),
    }


def reference(xT, w1, w2, gate, offs, dst):
    idx = unstriped(offs)
    xq = mxq(f64(xT)[:, idx], 0, "e4m3")
    h = relu2(by_expert(mxq(f64(w1), 1, "e4m3"), xq))
    y = by_expert(mxq(f64(w2), 1, "e4m3"), mxq(h, 0, "e4m3"))
    out = np.zeros((N, T))
    out[:, unstriped(dst)] = f64(gate) * y
    return out

@@ -1,0 +1,240 @@
+from contextlib import ExitStack
+
+import concourse.mybir as mybir
+
+K, T, E, C, H, N = 1536, 1024, 6, 128, 512, 256
+FLOPS = 2 * E * C * (K * H + H * N)
+
+F32 = mybir.dt.float32
+BF16 = mybir.dt.bfloat16
+U32 = mybir.dt.uint32
+U16 = mybir.dt.uint16
+U8 = mybir.dt.uint8
+FP8X4 = mybir.dt.float8_e4m3fn_x4
+RELU = mybir.ActivationFunctionType.Relu
+SQUARE = mybir.ActivationFunctionType.Square
+MULT = mybir.AluOpType.mult
+
+P = 128
+PACK = 4
+PASS = P * PACK
+PASSES = K // PASS
+SLOTS = E * C
+HALVES = N // P
+LAST = E - 1
+WIDTH = 512
+AHEAD = 8
+LIST_ROWS = 16
+
+X_COPIERS = ("SV", "S", "V", "S", "S", "VS")
+W1_COPIERS = ("S", "V", "S")
+W1_LAST_COPIERS = ("S", "V", "SV")
+W2_COPIERS = ("V", "V", "V", "V", "S", "S")
+
+
+def tile_moe_two_mlp_relu2_kernel(tc, xT, w1, w2, gate, offs, dst, out):
+    nc = tc.nc
+
+    jobs = []
+    for i, copiers in enumerate(X_COPIERS):
+        jobs.append(("x", 0, i * WIDTH // T, i * WIDTH % T, WIDTH, copiers))
+    for e in range(E):
+        for s in range(PASSES):
+            copiers = W1_LAST_COPIERS[s] if e == LAST else W1_COPIERS[s]
+            jobs.append(("w1", e, s, 0, H, copiers))
+            if s == 0 and 0 < e < LAST:
+                jobs.append(("w2", e - 1, 0, 0, N, W2_COPIERS[e - 1]))
+    for e in (LAST - 1, LAST):
+        jobs.append(("w2", e, 0, 0, N, W2_COPIERS[e]))
+
+    with ExitStack() as ctx:
+        keep = ctx.enter_context(tc.tile_pool(name="keep", bufs=1))
+        raw_pool = ctx.enter_context(tc.tile_pool(name="raw", bufs=AHEAD + 4))
+        raw2_pool = ctx.enter_context(tc.tile_pool(name="raw2", bufs=3))
+        grouped_pool = ctx.enter_context(tc.tile_pool(name="grouped", bufs=6))
+        code_pool = ctx.enter_context(tc.tile_pool(name="codes", bufs=8))
+        small_pool = ctx.enter_context(tc.tile_pool(name="small", bufs=3))
+        sum_psum = ctx.enter_context(tc.psum_pool(name="sum_psum", bufs=2))
+        last_psum = ctx.enter_context(tc.psum_pool(name="last_psum", bufs=1))
+        y_psum = ctx.enter_context(tc.psum_pool(name="y_psum", bufs=1))
+
+        offs_sb = keep.tile([P, SLOTS // LIST_ROWS], U16, name="offs_sb")
+        dst_sb = keep.tile([P, SLOTS // LIST_ROWS], U16, name="dst_sb")
+        gate_sb = keep.tile([P, SLOTS], F32, name="gate_sb")
+        x_codes = [keep.tile([P, T], U32, name=f"x_codes{s}", align_bytes=64) for s in range(PASSES)]
+        x_scales = keep.tile([P, T], U8, name="x_scales", align_bytes=64)
+        slot_codes = [keep.tile([P, SLOTS], U32, name=f"slot_codes{s}", align_bytes=64) for s in range(PASSES)]
+        slot_scales = keep.tile([P, SLOTS], U8, name="slot_scales", align_bytes=64)
+        out_sb = [keep.tile([P, T], F32, name=f"out_sb{half}") for half in range(HALVES)]
+
+        nc.gpsimd.memset(x_scales[:], 0)
+        for half in range(HALVES):
+            nc.gpsimd.memset(out_sb[half][:], 0.0)
+
+        raws, grouped, weights, hidden, sums, results = {}, {}, {}, {}, {}, {}
+
+        def load(i):
+            tensor, e, s, first, width, copiers = jobs[i]
+            part = width // len(copiers)
+            raws[i] = []
+            for c0 in range(first, first + width, part):
+                if tensor == "x":
+                    raw = raw_pool.tile([P, PACK, part], F32, name="raw")
+                    src = xT[s * PASS : (s + 1) * PASS, c0 : c0 + part]
+                elif tensor == "w1":
+                    raw = raw_pool.tile([P, PACK, part], F32, name="raw")
+                    src = w1[e, s * PASS : (s + 1) * PASS, c0 : c0 + part]
+                else:
+                    raw = raw2_pool.tile([P, PACK, part], F32, name="raw2")
+                    src = w2[e, :, c0 : c0 + part]
+                nc.sync.dma_start(out=raw[:], in_=src.rearrange("(p j) c -> p j c", j=PACK))
+                raws[i].append(raw)
+            if i == 0:
+                nc.sync.dma_start(offs_sb[:], offs)
+            if i == AHEAD + 3:
+                nc.sync.dma_start(dst_sb[:], dst)
+                nc.sync.dma_start(out=gate_sb[:], in_=gate[0:P, :])
+
+        def copy(i):
+            tensor, e, s, first, width, copiers = jobs[i]
+            part = width // len(copiers)
+            tile = grouped_pool.tile(
+                [P, width * PACK], BF16, name="grouped2" if tensor == "w2" else "grouped", align_bytes=64
+            )
+            for n, (copier, raw) in enumerate(zip(copiers, raws.pop(i))):
+                if tensor == "w1":
+                    src = raw[:].rearrange("p j (m t) -> p m j t", t=PACK)
+                    dest = tile[:].rearrange("p (t m j) -> p m j t", t=PACK, j=PACK)
+                    dest = dest[:, n * part // PACK : (n + 1) * part // PACK]
+                else:
+                    src = raw[:].rearrange("p j (c i) -> p c j i", i=4)
+                    dest = tile[:, n * part * PACK : (n + 1) * part * PACK]
+                    dest = dest.rearrange("p (c i j) -> p c j i", i=4, j=PACK)
+                if copier == "S":
+                    nc.scalar.copy(out=dest, in_=src)
+                else:
+                    nc.vector.tensor_copy(out=dest, in_=src)
+            grouped[i] = tile
+
+        def quantise(i):
+            tensor, e, s, first, width, copiers = jobs[i]
+            if tensor == "x":
+                codes = x_codes[s][:, first : first + width]
+                scales = x_scales[4 * s : P, first : first + width]
+            else:
+                codes = code_pool.tile([P, width], U32, name="codes_" + tensor, align_bytes=64)[:, :]
+                scales = code_pool.tile([P, width], U8, name="scales_" + tensor, align_bytes=64)[:, :]
+                weights[tensor, e, s] = (codes, scales)
+            nc.vector.quantize_mx(out=codes.bitcast(FP8X4), scales=scales, in_=grouped.pop(i)[:])
+
+        def gather(slots, table, first, end):
+            listed = offs_sb[:, first // LIST_ROWS : end // LIST_ROWS]
+            nc.vector.tensor_copy(slots[:, first:end], table[:].indirect(listed))
+
+        def gather_pass(s):
+            if s < PASSES - 1:
+                gather(slot_codes[s], x_codes[s], 0, SLOTS)
+                return
+            for first, end in ((0, 2 * C), (2 * C, SLOTS)):
+                gather(slot_codes[s], x_codes[s], first, end)
+                gather(slot_scales, x_scales, first, end)
+
+        def first_layer(e, group, s, into):
+            codes, scales = weights["w1", e, s]
+            chans = slice(group * P, (group + 1) * P)
+            slots = slice(e * C, (e + 1) * C)
+            nc.tensor.matmul_mx(
+                out=into,
+                lhsT=codes[:, chans].bitcast(FP8X4),
+                lhsT_scale=scales[:, chans],
+                rhs=slot_codes[s][:, slots].bitcast(FP8X4),
+                rhs_scale=slot_scales[4 * s : P, slots],
+                start=(s == 0),
+                stop=(s == PASSES - 1),
+            )
+
+        def first_layer_and_relu(e):
+            bank = sum_psum.tile([P, PACK, C], F32, name="bank")
+            for group in range(PACK):
+                for s in range(PASSES):
+                    first_layer(e, group, s, bank[:, group, :])
+            relu = small_pool.tile([P, PACK, C], F32, name="relu")
+            nc.scalar.activation(relu[:], bank[:], RELU)
+            return relu
+
+        def last_first_layer(s):
+            if s == 0:
+                for group in range(PACK):
+                    sums[group] = last_psum.tile([P, C], F32, name=f"last{group}")
+            for group in range(PACK):
+                first_layer(LAST, group, s, sums[group][:])
+
+        def last_relu():
+            relu = small_pool.tile([P, PACK, C], F32, name="relu")
+            for group in range(PACK):
+                if group % 2 == 0:
+                    nc.scalar.activation(relu[:, group, :], sums[group][:], RELU)
+                else:
+                    nc.vector.tensor_scalar_max(relu[:, group, :], sums[group][:], 0.0)
+            return relu
+
+        def square_and_quantise(e, relu):
+            tile = small_pool.tile([P, C * PACK], BF16, name="h", align_bytes=64)
+            h = tile[:].rearrange("p (c t) -> p c t", t=PACK)
+            r = relu[:].rearrange("p t c -> p c t")
+            if e < LAST:
+                nc.scalar.activation(h, r, SQUARE)
+            else:
+                nc.scalar.activation(h[:, 0 : C // 2], r[:, 0 : C // 2], SQUARE)
+                nc.vector.tensor_tensor(h[:, C // 2 :], r[:, C // 2 :], r[:, C // 2 :], MULT)
+            codes = small_pool.tile([P, C], U32, name="h_codes", align_bytes=64)
+            scales = small_pool.tile([P, C], U8, name="h_scales", align_bytes=64)
+            nc.vector.quantize_mx(out=codes[:].bitcast(FP8X4), scales=scales[:], in_=tile[:])
+            hidden[e] = (codes, scales)
+
+        def second_layer(e):
+            w_codes, w_scales = weights["w2", e, 0]
+            h_codes, h_scales = hidden[e]
+            for members in [range(HALVES)] if e < LAST else [[half] for half in range(HALVES)]:
+                y = y_psum.tile([P, len(members), C], F32, name=f"y{members[0]}")
+                for n, half in enumerate(members):
+                    chans = slice(half * P, (half + 1) * P)
+                    nc.tensor.matmul_mx(
+                        out=y[:, n, :],
+                        lhsT=w_codes[:, chans].bitcast(FP8X4),
+                        lhsT_scale=w_scales[:, chans],
+                        rhs=h_codes[:].bitcast(FP8X4),
+                        rhs_scale=h_scales[:],
+                        start=True,
+                        stop=True,
+                    )
+                y_sb = small_pool.tile([P, len(members), C], F32, name=f"y_sb{members[0]}")
+                nc.scalar.copy(out=y_sb[:], in_=y[:])
+                for n, half in enumerate(members):
+                    results[e, half] = y_sb[:, n, :]
+
+        def scatter(e):
+            listed = dst_sb[:, e * C // LIST_ROWS : (e + 1) * C // LIST_ROWS]
+            for half in range(HALVES):
+                nc.vector.tensor_tensor(
+                    out_sb[half][:].indirect(listed), results[e, half], gate_sb[:, e * C : (e + 1) * C], MULT
+                )
+                if e == LAST:
+                    nc.sync.dma_start(out=out[half * P : (half + 1) * P, :], in_=out_sb[half][:])
+
+        for i in range(AHEAD):
+            load(i)
+        for i, (tensor, e, s, first, width, copiers) in enumerate(jobs):
+            if i + AHEAD < len(jobs):
+                load(i + AHEAD)
+            copy(i)
+            quantise(i)
+            if tensor == "x" and first + width == T:
+                gather_pass(s)
+            if tensor == "w1" and e == LAST:
+                last_first_layer(s)
+            if tensor == "w1" and s == PASSES - 1:
+                square_and_quantise(e, last_relu() if e == LAST else first_layer_and_relu(e))
+            if tensor == "w2":
+                second_layer(e)
+                scatter(e)

@@ -1,6 +1,7 @@
 from contextlib import ExitStack
 
 import concourse.mybir as mybir
+from concourse.masks import make_identity
 
 K, T, E, C, H, N = 1536, 1024, 6, 128, 512, 256
 FLOPS = 2 * E * C * (K * H + H * N)
@@ -23,36 +24,34 @@ SLOTS = E * C
 HALVES = N // P
 LAST = E - 1
 WIDTH = 512
-AHEAD = 8
+AHEAD = 6
+GATE_ROWS = 2
+GATE_BLOCKS = E // GATE_ROWS
 LIST_ROWS = 16
 
-X_COPIERS = ("SV", "S", "V", "S", "S", "VS")
-W1_COPIERS = ("S", "V", "S")
-W1_LAST_COPIERS = ("S", "V", "SV")
-W2_COPIERS = ("V", "V", "V", "V", "S", "S")
+X_COPIERS = ((("V", 512),), (("S", 512),))
+W1_COPIERS = ((("S", 512),), (("V", 512),), (("S", 512),))
+W1_SHARED = (("S", 256), ("V", 256))
+W2_COPIERS = ("V", "V", "V", "V", "S", "V")
 
 
 def tile_moe_two_mlp_relu2_kernel(tc, xT, w1, w2, gate, offs, dst, out):
     nc = tc.nc
 
-    jobs = []
-    for i, copiers in enumerate(X_COPIERS):
-        jobs.append(("x", 0, i * WIDTH // T, i * WIDTH % T, WIDTH, copiers))
-    for e in range(E):
+    loads = [("x", 0, 0), ("x", 0, 1), ("x", 0, 2), ("w1", 0, 0), ("w1", 0, 1), ("w1", 0, 2)]
+    for e in range(1, E):
         for s in range(PASSES):
-            copiers = W1_LAST_COPIERS[s] if e == LAST else W1_COPIERS[s]
-            jobs.append(("w1", e, s, 0, H, copiers))
-            if s == 0 and 0 < e < LAST:
-                jobs.append(("w2", e - 1, 0, 0, N, W2_COPIERS[e - 1]))
-    for e in (LAST - 1, LAST):
-        jobs.append(("w2", e, 0, 0, N, W2_COPIERS[e]))
+            loads.append(("w1", e, s))
+        loads.append(("w2", e - 1, 0))
+    loads.append(("w2", LAST, 0))
 
     with ExitStack() as ctx:
         keep = ctx.enter_context(tc.tile_pool(name="keep", bufs=1))
-        raw_pool = ctx.enter_context(tc.tile_pool(name="raw", bufs=AHEAD + 4))
+        raw_pool = ctx.enter_context(tc.tile_pool(name="raw", bufs=8))
+        rawx_pool = ctx.enter_context(tc.tile_pool(name="rawx", bufs=3))
         raw2_pool = ctx.enter_context(tc.tile_pool(name="raw2", bufs=3))
-        grouped_pool = ctx.enter_context(tc.tile_pool(name="grouped", bufs=6))
-        code_pool = ctx.enter_context(tc.tile_pool(name="codes", bufs=8))
+        grouped_pool = ctx.enter_context(tc.tile_pool(name="grouped", bufs=4))
+        code_pool = ctx.enter_context(tc.tile_pool(name="codes", bufs=6))
         small_pool = ctx.enter_context(tc.tile_pool(name="small", bufs=3))
         sum_psum = ctx.enter_context(tc.psum_pool(name="sum_psum", bufs=2))
         last_psum = ctx.enter_context(tc.psum_pool(name="last_psum", bufs=1))
@@ -67,57 +66,73 @@ def tile_moe_two_mlp_relu2_kernel(tc, xT, w1, w2, gate, offs, dst, out):
         slot_scales = keep.tile([P, SLOTS], U8, name="slot_scales", align_bytes=64)
         out_sb = [keep.tile([P, T], F32, name=f"out_sb{half}") for half in range(HALVES)]
 
-        nc.gpsimd.memset(x_scales[:], 0)
+        nc.vector.memset(x_scales[:], 0)
         for half in range(HALVES):
-            nc.gpsimd.memset(out_sb[half][:], 0.0)
+            nc.vector.memset(out_sb[half][:], 0.0)
 
-        raws, grouped, weights, hidden, sums, results = {}, {}, {}, {}, {}, {}
+        identity = keep.tile([P, P], F32, name="identity")
+        make_identity(nc, identity[:])
+        gate_rows = keep.tile([P, GATE_BLOCKS * C], F32, name="gate_rows")
+        nc.vector.memset(gate_rows[:], 0.0)
+
+        def spread_gate():
+            turned = last_psum.tile([P, GATE_BLOCKS, C], F32, name="last0")
+            for b in range(GATE_BLOCKS):
+                nc.tensor.transpose(turned[:, b, :], gate_rows[:, b * C : (b + 1) * C], identity[:])
+            columns = keep.tile([P, GATE_BLOCKS, GATE_ROWS], F32, name="gate_columns")
+            nc.scalar.copy(out=columns[:], in_=turned[:, :, 0:GATE_ROWS])
+            for r in range(GATE_ROWS):
+                spread = last_psum.tile([P, GATE_BLOCKS, C], F32, name=f"last{r + 1}")
+                for b in range(GATE_BLOCKS):
+                    nc.tensor.transpose(spread[:, b, :], columns[:, b, r : r + 1].to_broadcast([P, C]), identity[:])
+                width = GATE_BLOCKS * C
+                nc.scalar.copy(out=gate_sb[:, r * width : (r + 1) * width], in_=spread[:].rearrange("p b c -> p (b c)"))
+
+        raws, weights, hidden, sums, results = {}, {}, {}, {}, {}
 
         def load(i):
-            tensor, e, s, first, width, copiers = jobs[i]
-            part = width // len(copiers)
-            raws[i] = []
-            for c0 in range(first, first + width, part):
-                if tensor == "x":
-                    raw = raw_pool.tile([P, PACK, part], F32, name="raw")
-                    src = xT[s * PASS : (s + 1) * PASS, c0 : c0 + part]
-                elif tensor == "w1":
-                    raw = raw_pool.tile([P, PACK, part], F32, name="raw")
-                    src = w1[e, s * PASS : (s + 1) * PASS, c0 : c0 + part]
-                else:
-                    raw = raw2_pool.tile([P, PACK, part], F32, name="raw2")
-                    src = w2[e, :, c0 : c0 + part]
-                nc.sync.dma_start(out=raw[:], in_=src.rearrange("(p j) c -> p j c", j=PACK))
-                raws[i].append(raw)
+            tensor, e, s = loads[i]
+            if tensor == "x":
+                raw = rawx_pool.tile([P, PACK, T], F32, name="rawx")
+                src = xT[s * PASS : (s + 1) * PASS, :]
+            elif tensor == "w1":
+                raw = raw_pool.tile([P, PACK, H], F32, name="raw")
+                src = w1[e, s * PASS : (s + 1) * PASS, :]
+            else:
+                raw = raw2_pool.tile([P, PACK, N], F32, name="raw2")
+                src = w2[e]
+            nc.sync.dma_start(out=raw[:], in_=src.rearrange("(p j) c -> p j c", j=PACK))
+            raws[i] = raw
             if i == 0:
                 nc.sync.dma_start(offs_sb[:], offs)
-            if i == AHEAD + 3:
+                nc.sync.dma_start(
+                    out=gate_rows[0:GATE_ROWS, :], in_=gate[0:1, :].rearrange("o (r c) -> (o r) c", r=GATE_ROWS)
+                )
+            if i == 7:
                 nc.sync.dma_start(dst_sb[:], dst)
-                nc.sync.dma_start(out=gate_sb[:], in_=gate[0:P, :])
 
-        def copy(i):
-            tensor, e, s, first, width, copiers = jobs[i]
-            part = width // len(copiers)
+        def copy(tensor, raw, first, width, copiers):
             tile = grouped_pool.tile(
                 [P, width * PACK], BF16, name="grouped2" if tensor == "w2" else "grouped", align_bytes=64
             )
-            for n, (copier, raw) in enumerate(zip(copiers, raws.pop(i))):
+            c0 = 0
+            for copier, part in copiers:
                 if tensor == "w1":
-                    src = raw[:].rearrange("p j (m t) -> p m j t", t=PACK)
+                    src = raw[:, :, c0 : c0 + part].rearrange("p j (m t) -> p m j t", t=PACK)
                     dest = tile[:].rearrange("p (t m j) -> p m j t", t=PACK, j=PACK)
-                    dest = dest[:, n * part // PACK : (n + 1) * part // PACK]
+                    dest = dest[:, c0 // PACK : (c0 + part) // PACK]
                 else:
-                    src = raw[:].rearrange("p j (c i) -> p c j i", i=4)
-                    dest = tile[:, n * part * PACK : (n + 1) * part * PACK]
+                    src = raw[:, :, first + c0 : first + c0 + part].rearrange("p j (c i) -> p c j i", i=4)
+                    dest = tile[:, c0 * PACK : (c0 + part) * PACK]
                     dest = dest.rearrange("p (c i j) -> p c j i", i=4, j=PACK)
                 if copier == "S":
                     nc.scalar.copy(out=dest, in_=src)
                 else:
                     nc.vector.tensor_copy(out=dest, in_=src)
-            grouped[i] = tile
+                c0 = c0 + part
+            return tile
 
-        def quantise(i):
-            tensor, e, s, first, width, copiers = jobs[i]
+        def quantise(tensor, e, s, first, width, tile):
             if tensor == "x":
                 codes = x_codes[s][:, first : first + width]
                 scales = x_scales[4 * s : P, first : first + width]
@@ -125,7 +140,7 @@ def tile_moe_two_mlp_relu2_kernel(tc, xT, w1, w2, gate, offs, dst, out):
                 codes = code_pool.tile([P, width], U32, name="codes_" + tensor, align_bytes=64)[:, :]
                 scales = code_pool.tile([P, width], U8, name="scales_" + tensor, align_bytes=64)[:, :]
                 weights[tensor, e, s] = (codes, scales)
-            nc.vector.quantize_mx(out=codes.bitcast(FP8X4), scales=scales, in_=grouped.pop(i)[:])
+            nc.vector.quantize_mx(out=codes.bitcast(FP8X4), scales=scales, in_=tile[:])
 
         def gather(slots, table, first, end):
             listed = offs_sb[:, first // LIST_ROWS : end // LIST_ROWS]
@@ -172,7 +187,7 @@ def tile_moe_two_mlp_relu2_kernel(tc, xT, w1, w2, gate, offs, dst, out):
         def last_relu():
             relu = small_pool.tile([P, PACK, C], F32, name="relu")
             for group in range(PACK):
-                if group % 2 == 0:
+                if group < PACK // 2:
                     nc.scalar.activation(relu[:, group, :], sums[group][:], RELU)
                 else:
                     nc.vector.tensor_scalar_max(relu[:, group, :], sums[group][:], 0.0)
@@ -224,17 +239,25 @@ def tile_moe_two_mlp_relu2_kernel(tc, xT, w1, w2, gate, offs, dst, out):
 
         for i in range(AHEAD):
             load(i)
-        for i, (tensor, e, s, first, width, copiers) in enumerate(jobs):
-            if i + AHEAD < len(jobs):
+        for i, (tensor, e, s) in enumerate(loads):
+            if i + AHEAD < len(loads):
                 load(i + AHEAD)
-            copy(i)
-            quantise(i)
-            if tensor == "x" and first + width == T:
+            raw = raws.pop(i)
+            if i == 1:
+                spread_gate()
+            if tensor == "x":
+                tiles = [copy(tensor, raw, n * WIDTH, WIDTH, copiers) for n, copiers in enumerate(X_COPIERS)]
+                for n, tile in enumerate(tiles):
+                    quantise(tensor, e, s, n * WIDTH, WIDTH, tile)
                 gather_pass(s)
-            if tensor == "w1" and e == LAST:
-                last_first_layer(s)
-            if tensor == "w1" and s == PASSES - 1:
-                square_and_quantise(e, last_relu() if e == LAST else first_layer_and_relu(e))
-            if tensor == "w2":
+            elif tensor == "w1":
+                shared = (e, s) == (LAST, PASSES - 1)
+                quantise(tensor, e, s, 0, H, copy(tensor, raw, 0, H, W1_SHARED if shared else W1_COPIERS[s]))
+                if e == LAST:
+                    last_first_layer(s)
+                if s == PASSES - 1:
+                    square_and_quantise(e, last_relu() if e == LAST else first_layer_and_relu(e))
+            else:
+                quantise(tensor, e, s, 0, N, copy(tensor, raw, 0, N, ((W2_COPIERS[e], N),)))
                 second_layer(e)
                 scatter(e)

@@ -31,7 +31,6 @@ LIST_ROWS = 16
 
 X_COPIERS = ((("V", 512),), (("S", 512),))
 W1_COPIERS = ((("S", 512),), (("V", 512),), (("S", 512),))
-W1_SHARED = (("S", 256), ("V", 256))
 W2_COPIERS = ("V", "V", "V", "V", "S", "V")
 
 
@@ -118,9 +117,8 @@ def tile_moe_two_mlp_relu2_kernel(tc, xT, w1, w2, gate, offs, dst, out):
             c0 = 0
             for copier, part in copiers:
                 if tensor == "w1":
-                    src = raw[:, :, c0 : c0 + part].rearrange("p j (m t) -> p m j t", t=PACK)
-                    dest = tile[:].rearrange("p (t m j) -> p m j t", t=PACK, j=PACK)
-                    dest = dest[:, c0 // PACK : (c0 + part) // PACK]
+                    src = raw[:].rearrange("p j (m u v) -> p u m j v", u=2, v=2)
+                    dest = tile[:].rearrange("p (u v m j) -> p u m j v", u=2, v=2, j=PACK)
                 else:
                     src = raw[:, :, first + c0 : first + c0 + part].rearrange("p j (c i) -> p c j i", i=4)
                     dest = tile[:, c0 * PACK : (c0 + part) * PACK]
@@ -131,6 +129,21 @@ def tile_moe_two_mlp_relu2_kernel(tc, xT, w1, w2, gate, offs, dst, out):
                     nc.vector.tensor_copy(out=dest, in_=src)
                 c0 = c0 + part
             return tile
+
+        def last_pass(raw):
+            codes = code_pool.tile([P, H], U32, name="codes_w1", align_bytes=64)[:, :]
+            scales = code_pool.tile([P, H], U8, name="scales_w1", align_bytes=64)[:, :]
+            weights["w1", LAST, PASSES - 1] = (codes, scales)
+            src = raw[:].rearrange("p j (m u v) -> p u m j v", u=2, v=2)
+            tiles = [grouped_pool.tile([P, 2 * P * PACK], BF16, name="grouped2", align_bytes=64) for u in range(2)]
+            dests = [tile[:].rearrange("p (v m j) -> p m j v", v=2, j=PACK) for tile in tiles]
+            nc.vector.tensor_copy(out=dests[0], in_=src[:, 0])
+            nc.scalar.copy(out=dests[1], in_=src[:, 1])
+            for u in range(2):
+                chans = slice(2 * u * P, 2 * (u + 1) * P)
+                nc.vector.quantize_mx(out=codes[:, chans].bitcast(FP8X4), scales=scales[:, chans], in_=tiles[u][:])
+                for group in (2 * u, 2 * u + 1):
+                    first_layer(LAST, group, PASSES - 1, sums[group][:])
 
         def quantise(tensor, e, s, first, width, tile):
             if tensor == "x":
@@ -173,9 +186,9 @@ def tile_moe_two_mlp_relu2_kernel(tc, xT, w1, w2, gate, offs, dst, out):
             for group in range(PACK):
                 for s in range(PASSES):
                     first_layer(e, group, s, bank[:, group, :])
-            relu = small_pool.tile([P, PACK, C], F32, name="relu")
-            nc.scalar.activation(relu[:], bank[:], RELU)
-            return relu
+            relu = small_pool.tile([P, C, PACK], F32, name="relu")
+            nc.scalar.activation(relu[:], bank[:].rearrange("p t c -> p c t"), RELU)
+            return relu[:]
 
         def last_first_layer(s):
             if s == 0:
@@ -187,16 +200,12 @@ def tile_moe_two_mlp_relu2_kernel(tc, xT, w1, w2, gate, offs, dst, out):
         def last_relu():
             relu = small_pool.tile([P, PACK, C], F32, name="relu")
             for group in range(PACK):
-                if group < PACK // 2:
-                    nc.scalar.activation(relu[:, group, :], sums[group][:], RELU)
-                else:
-                    nc.vector.tensor_scalar_max(relu[:, group, :], sums[group][:], 0.0)
-            return relu
+                nc.scalar.activation(relu[:, group, :], sums[group][:], RELU)
+            return relu[:].rearrange("p t c -> p c t")
 
-        def square_and_quantise(e, relu):
+        def square_and_quantise(e, r):
             tile = small_pool.tile([P, C * PACK], BF16, name="h", align_bytes=64)
             h = tile[:].rearrange("p (c t) -> p c t", t=PACK)
-            r = relu[:].rearrange("p t c -> p c t")
             if e < LAST:
                 nc.scalar.activation(h, r, SQUARE)
             else:
@@ -251,10 +260,12 @@ def tile_moe_two_mlp_relu2_kernel(tc, xT, w1, w2, gate, offs, dst, out):
                     quantise(tensor, e, s, n * WIDTH, WIDTH, tile)
                 gather_pass(s)
             elif tensor == "w1":
-                shared = (e, s) == (LAST, PASSES - 1)
-                quantise(tensor, e, s, 0, H, copy(tensor, raw, 0, H, W1_SHARED if shared else W1_COPIERS[s]))
-                if e == LAST:
-                    last_first_layer(s)
+                if (e, s) == (LAST, PASSES - 1):
+                    last_pass(raw)
+                else:
+                    quantise(tensor, e, s, 0, H, copy(tensor, raw, 0, H, W1_COPIERS[s]))
+                    if e == LAST:
+                        last_first_layer(s)
                 if s == PASSES - 1:
                     square_and_quantise(e, last_relu() if e == LAST else first_layer_and_relu(e))
             else:

@@ -31,7 +31,7 @@ LIST_ROWS = 16
 
 X_COPIERS = ((("V", 512),), (("S", 512),))
 W1_COPIERS = ((("S", 512),), (("V", 512),), (("S", 512),))
-W2_COPIERS = ("V", "V", "V", "V", "S", "V")
+W2_END_COPIERS = (("S", "S"), ("V", "V"))
 
 
 def tile_moe_two_mlp_relu2_kernel(tc, xT, w1, w2, gate, offs, dst, out):
@@ -52,6 +52,7 @@ def tile_moe_two_mlp_relu2_kernel(tc, xT, w1, w2, gate, offs, dst, out):
         grouped_pool = ctx.enter_context(tc.tile_pool(name="grouped", bufs=4))
         code_pool = ctx.enter_context(tc.tile_pool(name="codes", bufs=6))
         small_pool = ctx.enter_context(tc.tile_pool(name="small", bufs=3))
+        relu_pool = ctx.enter_context(tc.tile_pool(name="relu", bufs=1))
         sum_psum = ctx.enter_context(tc.psum_pool(name="sum_psum", bufs=2))
         last_psum = ctx.enter_context(tc.psum_pool(name="last_psum", bufs=1))
         y_psum = ctx.enter_context(tc.psum_pool(name="y_psum", bufs=1))
@@ -87,7 +88,7 @@ def tile_moe_two_mlp_relu2_kernel(tc, xT, w1, w2, gate, offs, dst, out):
                 width = GATE_BLOCKS * C
                 nc.scalar.copy(out=gate_sb[:, r * width : (r + 1) * width], in_=spread[:].rearrange("p b c -> p (b c)"))
 
-        raws, weights, hidden, sums, results = {}, {}, {}, {}, {}
+        raws, weights, hidden, sums = {}, {}, {}, {}
 
         def load(i):
             tensor, e, s = loads[i]
@@ -186,7 +187,7 @@ def tile_moe_two_mlp_relu2_kernel(tc, xT, w1, w2, gate, offs, dst, out):
             for group in range(PACK):
                 for s in range(PASSES):
                     first_layer(e, group, s, bank[:, group, :])
-            relu = small_pool.tile([P, C, PACK], F32, name="relu")
+            relu = relu_pool.tile([P, C, PACK], F32, name="relu")
             nc.scalar.activation(relu[:], bank[:].rearrange("p t c -> p c t"), RELU)
             return relu[:]
 
@@ -198,7 +199,7 @@ def tile_moe_two_mlp_relu2_kernel(tc, xT, w1, w2, gate, offs, dst, out):
                 first_layer(LAST, group, s, sums[group][:])
 
         def last_relu():
-            relu = small_pool.tile([P, PACK, C], F32, name="relu")
+            relu = relu_pool.tile([P, PACK, C], F32, name="relu")
             for group in range(PACK):
                 nc.scalar.activation(relu[:, group, :], sums[group][:], RELU)
             return relu[:].rearrange("p t c -> p c t")
@@ -206,42 +207,38 @@ def tile_moe_two_mlp_relu2_kernel(tc, xT, w1, w2, gate, offs, dst, out):
         def square_and_quantise(e, r):
             tile = small_pool.tile([P, C * PACK], BF16, name="h", align_bytes=64)
             h = tile[:].rearrange("p (c t) -> p c t", t=PACK)
-            if e < LAST:
-                nc.scalar.activation(h, r, SQUARE)
-            else:
-                nc.scalar.activation(h[:, 0 : C // 2], r[:, 0 : C // 2], SQUARE)
-                nc.vector.tensor_tensor(h[:, C // 2 :], r[:, C // 2 :], r[:, C // 2 :], MULT)
+            nc.scalar.activation(h, r, SQUARE)
             codes = small_pool.tile([P, C], U32, name="h_codes", align_bytes=64)
             scales = small_pool.tile([P, C], U8, name="h_scales", align_bytes=64)
             nc.vector.quantize_mx(out=codes[:].bitcast(FP8X4), scales=scales[:], in_=tile[:])
             hidden[e] = (codes, scales)
 
-        def second_layer(e):
+        def second_layer(e, raw, halves, copier):
+            first, width = halves[0] * P, len(halves) * P
+            quantise("w2", e, 0, first, width, copy("w2", raw, first, width, ((copier, width),)))
             w_codes, w_scales = weights["w2", e, 0]
             h_codes, h_scales = hidden[e]
-            for members in [range(HALVES)] if e < LAST else [[half] for half in range(HALVES)]:
-                y = y_psum.tile([P, len(members), C], F32, name=f"y{members[0]}")
-                for n, half in enumerate(members):
-                    chans = slice(half * P, (half + 1) * P)
-                    nc.tensor.matmul_mx(
-                        out=y[:, n, :],
-                        lhsT=w_codes[:, chans].bitcast(FP8X4),
-                        lhsT_scale=w_scales[:, chans],
-                        rhs=h_codes[:].bitcast(FP8X4),
-                        rhs_scale=h_scales[:],
-                        start=True,
-                        stop=True,
-                    )
-                y_sb = small_pool.tile([P, len(members), C], F32, name=f"y_sb{members[0]}")
-                nc.scalar.copy(out=y_sb[:], in_=y[:])
-                for n, half in enumerate(members):
-                    results[e, half] = y_sb[:, n, :]
-
-        def scatter(e):
+            y = y_psum.tile([P, len(halves), C], F32, name=f"y{halves[0]}")
+            for n in range(len(halves)):
+                chans = slice(n * P, (n + 1) * P)
+                nc.tensor.matmul_mx(
+                    out=y[:, n, :],
+                    lhsT=w_codes[:, chans].bitcast(FP8X4),
+                    lhsT_scale=w_scales[:, chans],
+                    rhs=h_codes[:].bitcast(FP8X4),
+                    rhs_scale=h_scales[:],
+                    start=True,
+                    stop=True,
+                )
+            if (e, halves[0]) == (LAST - 1, 1):
+                y_sb = relu_pool.tile([P, len(halves), C], F32, name="relu")
+            else:
+                y_sb = small_pool.tile([P, len(halves), C], F32, name=f"y_sb{halves[0]}")
+            nc.scalar.copy(out=y_sb[:], in_=y[:])
             listed = dst_sb[:, e * C // LIST_ROWS : (e + 1) * C // LIST_ROWS]
-            for half in range(HALVES):
+            for n, half in enumerate(halves):
                 nc.vector.tensor_tensor(
-                    out_sb[half][:].indirect(listed), results[e, half], gate_sb[:, e * C : (e + 1) * C], MULT
+                    out_sb[half][:].indirect(listed), y_sb[:, n, :], gate_sb[:, e * C : (e + 1) * C], MULT
                 )
                 if e == LAST:
                     nc.sync.dma_start(out=out[half * P : (half + 1) * P, :], in_=out_sb[half][:])
@@ -269,6 +266,8 @@ def tile_moe_two_mlp_relu2_kernel(tc, xT, w1, w2, gate, offs, dst, out):
                 if s == PASSES - 1:
                     square_and_quantise(e, last_relu() if e == LAST else first_layer_and_relu(e))
             else:
-                quantise(tensor, e, s, 0, N, copy(tensor, raw, 0, N, ((W2_COPIERS[e], N),)))
-                second_layer(e)
-                scatter(e)
+                if e < LAST - 1:
+                    second_layer(e, raw, range(HALVES), "V")
+                else:
+                    for half in range(HALVES):
+                        second_layer(e, raw, [half], W2_END_COPIERS[e - LAST + 1][half])

@@ -31,7 +31,7 @@ LIST_ROWS = 16
 
 X_COPIERS = ((("V", 512),), (("S", 512),))
 W1_COPIERS = ((("S", 512),), (("V", 512),), (("S", 512),))
-W2_END_COPIERS = (("S", "S"), ("V", "V"))
+W2_END_COPIERS = (("V", "S"), ("V", "S"))
 
 
 def tile_moe_two_mlp_relu2_kernel(tc, xT, w1, w2, gate, offs, dst, out):
@@ -131,12 +131,15 @@ def tile_moe_two_mlp_relu2_kernel(tc, xT, w1, w2, gate, offs, dst, out):
                 c0 = c0 + part
             return tile
 
-        def last_pass(raw):
+        def last_pass(s, raw):
             codes = code_pool.tile([P, H], U32, name="codes_w1", align_bytes=64)[:, :]
             scales = code_pool.tile([P, H], U8, name="scales_w1", align_bytes=64)[:, :]
-            weights["w1", LAST, PASSES - 1] = (codes, scales)
+            weights["w1", LAST, s] = (codes, scales)
+            if s == 0:
+                for group in range(PACK):
+                    sums[group] = last_psum.tile([P, C], F32, name=f"last{group}")
             src = raw[:].rearrange("p j (m u v) -> p u m j v", u=2, v=2)
-            tiles = [grouped_pool.tile([P, 2 * P * PACK], BF16, name="grouped2", align_bytes=64) for u in range(2)]
+            tiles = [grouped_pool.tile([P, 2 * P * PACK], BF16, name="grouped3", align_bytes=64) for u in range(2)]
             dests = [tile[:].rearrange("p (v m j) -> p m j v", v=2, j=PACK) for tile in tiles]
             nc.vector.tensor_copy(out=dests[0], in_=src[:, 0])
             nc.scalar.copy(out=dests[1], in_=src[:, 1])
@@ -144,7 +147,7 @@ def tile_moe_two_mlp_relu2_kernel(tc, xT, w1, w2, gate, offs, dst, out):
                 chans = slice(2 * u * P, 2 * (u + 1) * P)
                 nc.vector.quantize_mx(out=codes[:, chans].bitcast(FP8X4), scales=scales[:, chans], in_=tiles[u][:])
                 for group in (2 * u, 2 * u + 1):
-                    first_layer(LAST, group, PASSES - 1, sums[group][:])
+                    first_layer(LAST, group, s, sums[group][:])
 
         def quantise(tensor, e, s, first, width, tile):
             if tensor == "x":
@@ -190,13 +193,6 @@ def tile_moe_two_mlp_relu2_kernel(tc, xT, w1, w2, gate, offs, dst, out):
             relu = relu_pool.tile([P, C, PACK], F32, name="relu")
             nc.scalar.activation(relu[:], bank[:].rearrange("p t c -> p c t"), RELU)
             return relu[:]
-
-        def last_first_layer(s):
-            if s == 0:
-                for group in range(PACK):
-                    sums[group] = last_psum.tile([P, C], F32, name=f"last{group}")
-            for group in range(PACK):
-                first_layer(LAST, group, s, sums[group][:])
 
         def last_relu():
             relu = relu_pool.tile([P, PACK, C], F32, name="relu")
@@ -257,12 +253,10 @@ def tile_moe_two_mlp_relu2_kernel(tc, xT, w1, w2, gate, offs, dst, out):
                     quantise(tensor, e, s, n * WIDTH, WIDTH, tile)
                 gather_pass(s)
             elif tensor == "w1":
-                if (e, s) == (LAST, PASSES - 1):
-                    last_pass(raw)
+                if e == LAST:
+                    last_pass(s, raw)
                 else:
                     quantise(tensor, e, s, 0, H, copy(tensor, raw, 0, H, W1_COPIERS[s]))
-                    if e == LAST:
-                        last_first_layer(s)
                 if s == PASSES - 1:
                     square_and_quantise(e, last_relu() if e == LAST else first_layer_and_relu(e))
             else:

@@ -64,7 +64,7 @@ def tile_moe_two_mlp_relu2_kernel(tc, xT, w1, w2, gate, offs, dst, out):
         x_scales = keep.tile([P, T], U8, name="x_scales", align_bytes=64)
         slot_codes = [keep.tile([P, SLOTS], U32, name=f"slot_codes{s}", align_bytes=64) for s in range(PASSES)]
         slot_scales = keep.tile([P, SLOTS], U8, name="slot_scales", align_bytes=64)
-        out_sb = [keep.tile([P, T], F32, name=f"out_sb{half}") for half in range(HALVES)]
+        out_sb = [keep.tile([P, T], F32, name=f"out_sb{half}", align_bytes=256) for half in range(HALVES)]
 
         nc.vector.memset(x_scales[:], 0)
         for half in range(HALVES):
@@ -93,13 +93,13 @@ def tile_moe_two_mlp_relu2_kernel(tc, xT, w1, w2, gate, offs, dst, out):
         def load(i):
             tensor, e, s = loads[i]
             if tensor == "x":
-                raw = rawx_pool.tile([P, PACK, T], F32, name="rawx")
+                raw = rawx_pool.tile([P, PACK, T], F32, name="rawx", align_bytes=256)
                 src = xT[s * PASS : (s + 1) * PASS, :]
             elif tensor == "w1":
-                raw = raw_pool.tile([P, PACK, H], F32, name="raw")
+                raw = raw_pool.tile([P, PACK, H], F32, name="raw", align_bytes=256)
                 src = w1[e, s * PASS : (s + 1) * PASS, :]
             else:
-                raw = raw2_pool.tile([P, PACK, N], F32, name="raw2")
+                raw = raw2_pool.tile([P, PACK, N], F32, name="raw2", align_bytes=256)
                 src = w2[e]
             nc.sync.dma_start(out=raw[:], in_=src.rearrange("(p j) c -> p j c", j=PACK))
             raws[i] = raw

@@ -28,29 +28,33 @@ AHEAD = 6
 GATE_ROWS = 2
 GATE_BLOCKS = E // GATE_ROWS
 LIST_ROWS = 16
+MX_ALIGN = 256
+DMA_ALIGN = 256
 
-X_COPIERS = ((("V", 512),), (("S", 512),))
-W1_COPIERS = ((("S", 512),), (("V", 512),), (("S", 512),))
-W2_END_COPIERS = (("V", "S"), ("V", "S"))
+X_COPIERS = ("V", "S")
+W1_COPIERS = ("S", "V", "S")
+W2_COPIER = "V"
+W2_END_COPIERS = ("V", "S")
 
 
 def tile_moe_two_mlp_relu2_kernel(tc, xT, w1, w2, gate, offs, dst, out):
     nc = tc.nc
 
-    loads = [("x", 0, 0), ("x", 0, 1), ("x", 0, 2), ("w1", 0, 0), ("w1", 0, 1), ("w1", 0, 2)]
-    for e in range(1, E):
-        for s in range(PASSES):
-            loads.append(("w1", e, s))
-        loads.append(("w2", e - 1, 0))
+    loads = [("x", 0, s) for s in range(PASSES)]
+    for e in range(E):
+        loads.extend(("w1", e, s) for s in range(PASSES))
+        if e > 0:
+            loads.append(("w2", e - 1, 0))
     loads.append(("w2", LAST, 0))
+    dst_behind = ("w1", 1, 1)
 
     with ExitStack() as ctx:
         keep = ctx.enter_context(tc.tile_pool(name="keep", bufs=1))
         raw_pool = ctx.enter_context(tc.tile_pool(name="raw", bufs=8))
-        rawx_pool = ctx.enter_context(tc.tile_pool(name="rawx", bufs=3))
+        rawx_pool = ctx.enter_context(tc.tile_pool(name="rawx", bufs=PASSES))
         raw2_pool = ctx.enter_context(tc.tile_pool(name="raw2", bufs=3))
         grouped_pool = ctx.enter_context(tc.tile_pool(name="grouped", bufs=4))
-        code_pool = ctx.enter_context(tc.tile_pool(name="codes", bufs=6))
+        code_pool = ctx.enter_context(tc.tile_pool(name="codes", bufs=2 * PASSES))
         small_pool = ctx.enter_context(tc.tile_pool(name="small", bufs=3))
         relu_pool = ctx.enter_context(tc.tile_pool(name="relu", bufs=1))
         sum_psum = ctx.enter_context(tc.psum_pool(name="sum_psum", bufs=2))
@@ -60,11 +64,11 @@ def tile_moe_two_mlp_relu2_kernel(tc, xT, w1, w2, gate, offs, dst, out):
         offs_sb = keep.tile([P, SLOTS // LIST_ROWS], U16, name="offs_sb")
         dst_sb = keep.tile([P, SLOTS // LIST_ROWS], U16, name="dst_sb")
         gate_sb = keep.tile([P, SLOTS], F32, name="gate_sb")
-        x_codes = [keep.tile([P, T], U32, name=f"x_codes{s}", align_bytes=64) for s in range(PASSES)]
-        x_scales = keep.tile([P, T], U8, name="x_scales", align_bytes=64)
-        slot_codes = [keep.tile([P, SLOTS], U32, name=f"slot_codes{s}", align_bytes=64) for s in range(PASSES)]
-        slot_scales = keep.tile([P, SLOTS], U8, name="slot_scales", align_bytes=64)
-        out_sb = [keep.tile([P, T], F32, name=f"out_sb{half}", align_bytes=256) for half in range(HALVES)]
+        x_codes = [keep.tile([P, T], U32, name=f"x_codes{s}", align_bytes=MX_ALIGN) for s in range(PASSES)]
+        x_scales = keep.tile([P, T], U8, name="x_scales", align_bytes=MX_ALIGN)
+        slot_codes = [keep.tile([P, SLOTS], U32, name=f"slot_codes{s}", align_bytes=MX_ALIGN) for s in range(PASSES)]
+        slot_scales = keep.tile([P, SLOTS], U8, name="slot_scales", align_bytes=MX_ALIGN)
+        out_sb = [keep.tile([P, T], F32, name=f"out_sb{half}", align_bytes=DMA_ALIGN) for half in range(HALVES)]
 
         nc.vector.memset(x_scales[:], 0)
         for half in range(HALVES):
@@ -93,13 +97,13 @@ def tile_moe_two_mlp_relu2_kernel(tc, xT, w1, w2, gate, offs, dst, out):
         def load(i):
             tensor, e, s = loads[i]
             if tensor == "x":
-                raw = rawx_pool.tile([P, PACK, T], F32, name="rawx", align_bytes=256)
+                raw = rawx_pool.tile([P, PACK, T], F32, name="rawx", align_bytes=DMA_ALIGN)
                 src = xT[s * PASS : (s + 1) * PASS, :]
             elif tensor == "w1":
-                raw = raw_pool.tile([P, PACK, H], F32, name="raw", align_bytes=256)
+                raw = raw_pool.tile([P, PACK, H], F32, name="raw", align_bytes=DMA_ALIGN)
                 src = w1[e, s * PASS : (s + 1) * PASS, :]
             else:
-                raw = raw2_pool.tile([P, PACK, N], F32, name="raw2", align_bytes=256)
+                raw = raw2_pool.tile([P, PACK, N], F32, name="raw2", align_bytes=DMA_ALIGN)
                 src = w2[e]
             nc.sync.dma_start(out=raw[:], in_=src.rearrange("(p j) c -> p j c", j=PACK))
             raws[i] = raw
@@ -108,41 +112,39 @@ def tile_moe_two_mlp_relu2_kernel(tc, xT, w1, w2, gate, offs, dst, out):
                 nc.sync.dma_start(
                     out=gate_rows[0:GATE_ROWS, :], in_=gate[0:1, :].rearrange("o (r c) -> (o r) c", r=GATE_ROWS)
                 )
-            if i == 7:
+            if loads[i] == dst_behind:
                 nc.sync.dma_start(dst_sb[:], dst)
 
-        def copy(tensor, raw, first, width, copiers):
-            tile = grouped_pool.tile(
-                [P, width * PACK], BF16, name="grouped2" if tensor == "w2" else "grouped", align_bytes=64
-            )
-            c0 = 0
-            for copier, part in copiers:
-                if tensor == "w1":
-                    src = raw[:].rearrange("p j (m u v) -> p u m j v", u=2, v=2)
-                    dest = tile[:].rearrange("p (u v m j) -> p u m j v", u=2, v=2, j=PACK)
-                else:
-                    src = raw[:, :, first + c0 : first + c0 + part].rearrange("p j (c i) -> p c j i", i=4)
-                    dest = tile[:, c0 * PACK : (c0 + part) * PACK]
-                    dest = dest.rearrange("p (c i j) -> p c j i", i=4, j=PACK)
-                if copier == "S":
-                    nc.scalar.copy(out=dest, in_=src)
-                else:
-                    nc.vector.tensor_copy(out=dest, in_=src)
-                c0 = c0 + part
+        def move(copier, dest, src):
+            if copier == "S":
+                nc.scalar.copy(out=dest, in_=src)
+            else:
+                nc.vector.tensor_copy(out=dest, in_=src)
+
+        def interleave(raw, first, width, copier, tag):
+            tile = grouped_pool.tile([P, width * PACK], BF16, name=tag, align_bytes=MX_ALIGN)
+            src = raw[:, :, first : first + width].rearrange("p j (c i) -> p c j i", i=4)
+            move(copier, tile[:].rearrange("p (c i j) -> p c j i", i=4, j=PACK), src)
             return tile
 
-        def last_pass(s, raw):
-            codes = code_pool.tile([P, H], U32, name="codes_w1", align_bytes=64)[:, :]
-            scales = code_pool.tile([P, H], U8, name="scales_w1", align_bytes=64)[:, :]
+        def by_pairs(raw):
+            return raw[:].rearrange("p j (m u v) -> p u m j v", u=2, v=2)
+
+        def interleave_w1(raw, copier):
+            tile = grouped_pool.tile([P, H * PACK], BF16, name="grouped", align_bytes=MX_ALIGN)
+            move(copier, tile[:].rearrange("p (u v m j) -> p u m j v", u=2, v=2, j=PACK), by_pairs(raw))
+            return tile
+
+        def last_expert_pass(s, raw):
+            codes = code_pool.tile([P, H], U32, name="codes_w1", align_bytes=MX_ALIGN)[:, :]
+            scales = code_pool.tile([P, H], U8, name="scales_w1", align_bytes=MX_ALIGN)[:, :]
             weights["w1", LAST, s] = (codes, scales)
             if s == 0:
                 for group in range(PACK):
                     sums[group] = last_psum.tile([P, C], F32, name=f"last{group}")
-            src = raw[:].rearrange("p j (m u v) -> p u m j v", u=2, v=2)
-            tiles = [grouped_pool.tile([P, 2 * P * PACK], BF16, name="grouped3", align_bytes=64) for u in range(2)]
-            dests = [tile[:].rearrange("p (v m j) -> p m j v", v=2, j=PACK) for tile in tiles]
-            nc.vector.tensor_copy(out=dests[0], in_=src[:, 0])
-            nc.scalar.copy(out=dests[1], in_=src[:, 1])
+            tiles = [grouped_pool.tile([P, 2 * P * PACK], BF16, name="pair", align_bytes=MX_ALIGN) for u in range(2)]
+            for u, copier in enumerate(("V", "S")):
+                move(copier, tiles[u][:].rearrange("p (v m j) -> p m j v", v=2, j=PACK), by_pairs(raw)[:, u])
             for u in range(2):
                 chans = slice(2 * u * P, 2 * (u + 1) * P)
                 nc.vector.quantize_mx(out=codes[:, chans].bitcast(FP8X4), scales=scales[:, chans], in_=tiles[u][:])
@@ -154,8 +156,8 @@ def tile_moe_two_mlp_relu2_kernel(tc, xT, w1, w2, gate, offs, dst, out):
                 codes = x_codes[s][:, first : first + width]
                 scales = x_scales[4 * s : P, first : first + width]
             else:
-                codes = code_pool.tile([P, width], U32, name="codes_" + tensor, align_bytes=64)[:, :]
-                scales = code_pool.tile([P, width], U8, name="scales_" + tensor, align_bytes=64)[:, :]
+                codes = code_pool.tile([P, width], U32, name="codes_" + tensor, align_bytes=MX_ALIGN)[:, :]
+                scales = code_pool.tile([P, width], U8, name="scales_" + tensor, align_bytes=MX_ALIGN)[:, :]
                 weights[tensor, e, s] = (codes, scales)
             nc.vector.quantize_mx(out=codes.bitcast(FP8X4), scales=scales, in_=tile[:])
 
@@ -200,18 +202,18 @@ def tile_moe_two_mlp_relu2_kernel(tc, xT, w1, w2, gate, offs, dst, out):
                 nc.scalar.activation(relu[:, group, :], sums[group][:], RELU)
             return relu[:].rearrange("p t c -> p c t")
 
-        def square_and_quantise(e, r):
-            tile = small_pool.tile([P, C * PACK], BF16, name="h", align_bytes=64)
+        def square_and_quantise(e, relu):
+            tile = small_pool.tile([P, C * PACK], BF16, name="h", align_bytes=MX_ALIGN)
             h = tile[:].rearrange("p (c t) -> p c t", t=PACK)
-            nc.scalar.activation(h, r, SQUARE)
-            codes = small_pool.tile([P, C], U32, name="h_codes", align_bytes=64)
-            scales = small_pool.tile([P, C], U8, name="h_scales", align_bytes=64)
+            nc.scalar.activation(h, relu, SQUARE)
+            codes = small_pool.tile([P, C], U32, name="h_codes", align_bytes=MX_ALIGN)
+            scales = small_pool.tile([P, C], U8, name="h_scales", align_bytes=MX_ALIGN)
             nc.vector.quantize_mx(out=codes[:].bitcast(FP8X4), scales=scales[:], in_=tile[:])
             hidden[e] = (codes, scales)
 
         def second_layer(e, raw, halves, copier):
             first, width = halves[0] * P, len(halves) * P
-            quantise("w2", e, 0, first, width, copy("w2", raw, first, width, ((copier, width),)))
+            quantise("w2", e, 0, first, width, interleave(raw, first, width, copier, "grouped2"))
             w_codes, w_scales = weights["w2", e, 0]
             h_codes, h_scales = hidden[e]
             y = y_psum.tile([P, len(halves), C], F32, name=f"y{halves[0]}")
@@ -245,23 +247,22 @@ def tile_moe_two_mlp_relu2_kernel(tc, xT, w1, w2, gate, offs, dst, out):
             if i + AHEAD < len(loads):
                 load(i + AHEAD)
             raw = raws.pop(i)
-            if i == 1:
+            if (tensor, s) == ("x", 1):
                 spread_gate()
             if tensor == "x":
-                tiles = [copy(tensor, raw, n * WIDTH, WIDTH, copiers) for n, copiers in enumerate(X_COPIERS)]
+                tiles = [interleave(raw, n * WIDTH, WIDTH, copier, "grouped") for n, copier in enumerate(X_COPIERS)]
                 for n, tile in enumerate(tiles):
                     quantise(tensor, e, s, n * WIDTH, WIDTH, tile)
                 gather_pass(s)
             elif tensor == "w1":
                 if e == LAST:
-                    last_pass(s, raw)
+                    last_expert_pass(s, raw)
                 else:
-                    quantise(tensor, e, s, 0, H, copy(tensor, raw, 0, H, W1_COPIERS[s]))
+                    quantise(tensor, e, s, 0, H, interleave_w1(raw, W1_COPIERS[s]))
                 if s == PASSES - 1:
                     square_and_quantise(e, last_relu() if e == LAST else first_layer_and_relu(e))
+            elif e < LAST - 1:
+                second_layer(e, raw, range(HALVES), W2_COPIER)
             else:
-                if e < LAST - 1:
-                    second_layer(e, raw, range(HALVES), "V")
-                else:
-                    for half in range(HALVES):
-                        second_layer(e, raw, [half], W2_END_COPIERS[e - LAST + 1][half])
+                for half, copier in enumerate(W2_END_COPIERS):
+                    second_layer(e, raw, [half], copier)

@@ -24,6 +24,7 @@ SLOTS = E * C
 HALVES = N // P
 LAST = E - 1
 WIDTH = 512
+HELD = (LAST - 1,)
 AHEAD = 6
 GATE_ROWS = 2
 GATE_BLOCKS = E // GATE_ROWS
@@ -44,17 +45,17 @@ def tile_moe_two_mlp_relu2_kernel(tc, xT, w1, w2, gate, offs, dst, out):
     for e in range(E):
         loads.extend(("w1", e, s) for s in range(PASSES))
         if e > 0:
-            loads.append(("w2", e - 1, 0))
+            loads.insert(len(loads) - (e < LAST), ("w2", e - 1, 0))
     loads.append(("w2", LAST, 0))
-    dst_behind = ("w1", 1, 1)
+    joined = {(0, 0): 3, (1, 0): 2, (2, 0): 2, (3, 0): 2}
+    dst_behind = ("w2", 0, 0)
 
     with ExitStack() as ctx:
         keep = ctx.enter_context(tc.tile_pool(name="keep", bufs=1))
-        raw_pool = ctx.enter_context(tc.tile_pool(name="raw", bufs=8))
-        rawx_pool = ctx.enter_context(tc.tile_pool(name="rawx", bufs=PASSES))
+        raw_pool = ctx.enter_context(tc.tile_pool(name="raw", bufs=5))
         raw2_pool = ctx.enter_context(tc.tile_pool(name="raw2", bufs=3))
         grouped_pool = ctx.enter_context(tc.tile_pool(name="grouped", bufs=4))
-        code_pool = ctx.enter_context(tc.tile_pool(name="codes", bufs=2 * PASSES))
+        code_pool = ctx.enter_context(tc.tile_pool(name="codes", bufs=PASSES + 1))
         small_pool = ctx.enter_context(tc.tile_pool(name="small", bufs=3))
         relu_pool = ctx.enter_context(tc.tile_pool(name="relu", bufs=1))
         sum_psum = ctx.enter_context(tc.psum_pool(name="sum_psum", bufs=2))
@@ -96,8 +97,20 @@ def tile_moe_two_mlp_relu2_kernel(tc, xT, w1, w2, gate, offs, dst, out):
 
         def load(i):
             tensor, e, s = loads[i]
+            if i in raws:
+                return
+            if tensor == "w1" and (e, s) in joined:
+                count = joined[e, s]
+                raw = raw_pool.tile([P, count, PACK, H], F32, name="raw", align_bytes=DMA_ALIGN)
+                nc.sync.dma_start(
+                    out=raw[:].rearrange("p n j c -> p n (j c)"),
+                    in_=w1[e, s * PASS : (s + count) * PASS, :].rearrange("(n p j) c -> p n (j c)", n=count, j=PACK),
+                )
+                for n in range(count):
+                    raws[i + n] = raw[:, n]
+                return
             if tensor == "x":
-                raw = rawx_pool.tile([P, PACK, T], F32, name="rawx", align_bytes=DMA_ALIGN)
+                raw = raw_pool.tile([P, PACK, T], F32, name="raw", align_bytes=DMA_ALIGN)
                 src = xT[s * PASS : (s + 1) * PASS, :]
             elif tensor == "w1":
                 raw = raw_pool.tile([P, PACK, H], F32, name="raw", align_bytes=DMA_ALIGN)
@@ -106,7 +119,7 @@ def tile_moe_two_mlp_relu2_kernel(tc, xT, w1, w2, gate, offs, dst, out):
                 raw = raw2_pool.tile([P, PACK, N], F32, name="raw2", align_bytes=DMA_ALIGN)
                 src = w2[e]
             nc.sync.dma_start(out=raw[:], in_=src.rearrange("(p j) c -> p j c", j=PACK))
-            raws[i] = raw
+            raws[i] = raw[:]
             if i == 0:
                 nc.sync.dma_start(offs_sb[:], offs)
                 nc.sync.dma_start(
@@ -128,18 +141,18 @@ def tile_moe_two_mlp_relu2_kernel(tc, xT, w1, w2, gate, offs, dst, out):
             return tile
 
         def by_pairs(raw):
-            return raw[:].rearrange("p j (m u v) -> p u m j v", u=2, v=2)
+            return raw.rearrange("p j (m u v) -> p u m j v", u=2, v=2)
 
         def interleave_w1(raw, copier):
             tile = grouped_pool.tile([P, H * PACK], BF16, name="grouped", align_bytes=MX_ALIGN)
             move(copier, tile[:].rearrange("p (u v m j) -> p u m j v", u=2, v=2, j=PACK), by_pairs(raw))
             return tile
 
-        def last_expert_pass(s, raw):
+        def shared_pass(e, s, raw):
             codes = code_pool.tile([P, H], U32, name="codes_w1", align_bytes=MX_ALIGN)[:, :]
             scales = code_pool.tile([P, H], U8, name="scales_w1", align_bytes=MX_ALIGN)[:, :]
-            weights["w1", LAST, s] = (codes, scales)
-            if s == 0:
+            weights["w1", e, s] = (codes, scales)
+            if (e, s) == (LAST, 0):
                 for group in range(PACK):
                     sums[group] = last_psum.tile([P, C], F32, name=f"last{group}")
             tiles = [grouped_pool.tile([P, 2 * P * PACK], BF16, name="pair", align_bytes=MX_ALIGN) for u in range(2)]
@@ -149,7 +162,10 @@ def tile_moe_two_mlp_relu2_kernel(tc, xT, w1, w2, gate, offs, dst, out):
                 chans = slice(2 * u * P, 2 * (u + 1) * P)
                 nc.vector.quantize_mx(out=codes[:, chans].bitcast(FP8X4), scales=scales[:, chans], in_=tiles[u][:])
                 for group in (2 * u, 2 * u + 1):
-                    first_layer(LAST, group, s, sums[group][:])
+                    if e == LAST:
+                        first_layer(e, group, s, sums[group][:], s == 0, s == PASSES - 1)
+                    else:
+                        first_layer(e, group, s, sums["bank"][:, group, :], False, group == PACK - 1)
 
         def quantise(tensor, e, s, first, width, tile):
             if tensor == "x":
@@ -173,7 +189,7 @@ def tile_moe_two_mlp_relu2_kernel(tc, xT, w1, w2, gate, offs, dst, out):
                 gather(slot_codes[s], x_codes[s], first, end)
                 gather(slot_scales, x_scales, first, end)
 
-        def first_layer(e, group, s, into):
+        def first_layer(e, group, s, into, first, last):
             codes, scales = weights["w1", e, s]
             chans = slice(group * P, (group + 1) * P)
             slots = slice(e * C, (e + 1) * C)
@@ -183,18 +199,24 @@ def tile_moe_two_mlp_relu2_kernel(tc, xT, w1, w2, gate, offs, dst, out):
                 lhsT_scale=scales[:, chans],
                 rhs=slot_codes[s][:, slots].bitcast(FP8X4),
                 rhs_scale=slot_scales[4 * s : P, slots],
-                start=(s == 0),
-                stop=(s == PASSES - 1),
+                start=first,
+                stop=last,
             )
 
-        def first_layer_and_relu(e):
-            bank = sum_psum.tile([P, PACK, C], F32, name="bank")
+        def first_layer_pass(e, s):
+            if s == 0:
+                sums["bank"] = sum_psum.tile([P, PACK, C], F32, name="bank")
             for group in range(PACK):
-                for s in range(PASSES):
-                    first_layer(e, group, s, bank[:, group, :])
-            relu = relu_pool.tile([P, C, PACK], F32, name="relu")
-            nc.scalar.activation(relu[:], bank[:].rearrange("p t c -> p c t"), RELU)
-            return relu[:]
+                first, last = (s, group) == (0, 0), (s, group) == (PASSES - 1, PACK - 1)
+                first_layer(e, group, s, sums["bank"][:, group, :], first, last)
+
+        def bank_relu(bank, spent=None):
+            if spent is None:
+                relu = relu_pool.tile([P, C, PACK], F32, name="relu")[:]
+            else:
+                relu = spent[:, 0, :].rearrange("p (c t) -> p c t", t=PACK)
+            nc.scalar.activation(relu, bank[:].rearrange("p t c -> p c t"), RELU)
+            return relu
 
         def last_relu():
             relu = relu_pool.tile([P, PACK, C], F32, name="relu")
@@ -211,7 +233,7 @@ def tile_moe_two_mlp_relu2_kernel(tc, xT, w1, w2, gate, offs, dst, out):
             nc.vector.quantize_mx(out=codes[:].bitcast(FP8X4), scales=scales[:], in_=tile[:])
             hidden[e] = (codes, scales)
 
-        def second_layer(e, raw, halves, copier):
+        def products(e, raw, halves, copier):
             first, width = halves[0] * P, len(halves) * P
             quantise("w2", e, 0, first, width, interleave(raw, first, width, copier, "grouped2"))
             w_codes, w_scales = weights["w2", e, 0]
@@ -228,11 +250,16 @@ def tile_moe_two_mlp_relu2_kernel(tc, xT, w1, w2, gate, offs, dst, out):
                     start=True,
                     stop=True,
                 )
-            if (e, halves[0]) == (LAST - 1, 1):
+            return y
+
+        def scatter(e, halves, y, spent=None):
+            if spent is not None:
+                y_sb = spent[:, 0, 0 : len(halves) * C].rearrange("p (n c) -> p n c", c=C)
+            elif (e, halves[0]) == (LAST - 1, 1):
                 y_sb = relu_pool.tile([P, len(halves), C], F32, name="relu")
             else:
                 y_sb = small_pool.tile([P, len(halves), C], F32, name=f"y_sb{halves[0]}")
-            nc.scalar.copy(out=y_sb[:], in_=y[:])
+            nc.scalar.copy(out=y_sb[:, :, :], in_=y[:])
             listed = dst_sb[:, e * C // LIST_ROWS : (e + 1) * C // LIST_ROWS]
             for n, half in enumerate(halves):
                 nc.vector.tensor_tensor(
@@ -255,14 +282,21 @@ def tile_moe_two_mlp_relu2_kernel(tc, xT, w1, w2, gate, offs, dst, out):
                     quantise(tensor, e, s, n * WIDTH, WIDTH, tile)
                 gather_pass(s)
             elif tensor == "w1":
-                if e == LAST:
-                    last_expert_pass(s, raw)
+                if e == LAST or (e >= LAST - 2 and s == PASSES - 1):
+                    shared_pass(e, s, raw)
                 else:
                     quantise(tensor, e, s, 0, H, interleave_w1(raw, W1_COPIERS[s]))
-                if s == PASSES - 1:
-                    square_and_quantise(e, last_relu() if e == LAST else first_layer_and_relu(e))
+                    first_layer_pass(e, s)
+                if s == PASSES - 1 and 0 < e < LAST:
+                    scatter(e - 1, range(HALVES), waiting, raw)
+                if s == 0 and e in HELD:
+                    square_and_quantise(e - 1, bank_relu(full, raw))
+                if s == PASSES - 1 and e + 1 in HELD:
+                    full = sums["bank"]
+                elif s == PASSES - 1:
+                    square_and_quantise(e, last_relu() if e == LAST else bank_relu(sums["bank"]))
             elif e < LAST - 1:
-                second_layer(e, raw, range(HALVES), W2_COPIER)
+                waiting = products(e, raw, range(HALVES), "S" if e == LAST - 2 else W2_COPIER)
             else:
                 for half, copier in enumerate(W2_END_COPIERS):
-                    second_layer(e, raw, [half], copier)
+                    scatter(e, [half], products(e, raw, [half], copier))

@@ -47,7 +47,7 @@ def tile_moe_two_mlp_relu2_kernel(tc, xT, w1, w2, gate, offs, dst, out):
         if e > 0:
             loads.insert(len(loads) - (e < LAST), ("w2", e - 1, 0))
     loads.append(("w2", LAST, 0))
-    joined = {(0, 0): 3, (1, 0): 2, (2, 0): 2, (3, 0): 2}
+    joined = {(0, 0): 3, (1, 0): 2, (2, 0): 2}
     dst_behind = ("w2", 0, 0)
 
     with ExitStack() as ctx:

@@ -47,12 +47,12 @@ def tile_moe_two_mlp_relu2_kernel(tc, xT, w1, w2, gate, offs, dst, out):
         if e > 0:
             loads.insert(len(loads) - (e < LAST), ("w2", e - 1, 0))
     loads.append(("w2", LAST, 0))
-    joined = {(0, 0): 3, (1, 0): 2, (2, 0): 2}
     dst_behind = ("w2", 0, 0)
 
     with ExitStack() as ctx:
         keep = ctx.enter_context(tc.tile_pool(name="keep", bufs=1))
-        raw_pool = ctx.enter_context(tc.tile_pool(name="raw", bufs=5))
+        raw_pool = ctx.enter_context(tc.tile_pool(name="raw", bufs=8))
+        rawx_pool = ctx.enter_context(tc.tile_pool(name="rawx", bufs=PASSES))
         raw2_pool = ctx.enter_context(tc.tile_pool(name="raw2", bufs=3))
         grouped_pool = ctx.enter_context(tc.tile_pool(name="grouped", bufs=4))
         code_pool = ctx.enter_context(tc.tile_pool(name="codes", bufs=PASSES + 1))
@@ -97,20 +97,8 @@ def tile_moe_two_mlp_relu2_kernel(tc, xT, w1, w2, gate, offs, dst, out):
 
         def load(i):
             tensor, e, s = loads[i]
-            if i in raws:
-                return
-            if tensor == "w1" and (e, s) in joined:
-                count = joined[e, s]
-                raw = raw_pool.tile([P, count, PACK, H], F32, name="raw", align_bytes=DMA_ALIGN)
-                nc.sync.dma_start(
-                    out=raw[:].rearrange("p n j c -> p n (j c)"),
-                    in_=w1[e, s * PASS : (s + count) * PASS, :].rearrange("(n p j) c -> p n (j c)", n=count, j=PACK),
-                )
-                for n in range(count):
-                    raws[i + n] = raw[:, n]
-                return
             if tensor == "x":
-                raw = raw_pool.tile([P, PACK, T], F32, name="raw", align_bytes=DMA_ALIGN)
+                raw = rawx_pool.tile([P, PACK, T], F32, name="rawx", align_bytes=DMA_ALIGN)
                 src = xT[s * PASS : (s + 1) * PASS, :]
             elif tensor == "w1":
                 raw = raw_pool.tile([P, PACK, H], F32, name="raw", align_bytes=DMA_ALIGN)

@@ -24,7 +24,6 @@ SLOTS = E * C
 HALVES = N // P
 LAST = E - 1
 WIDTH = 512
-HELD = (LAST - 1,)
 AHEAD = 6
 GATE_ROWS = 2
 GATE_BLOCKS = E // GATE_ROWS
@@ -33,8 +32,9 @@ MX_ALIGN = 256
 DMA_ALIGN = 256
 
 X_COPIERS = ("V", "S")
-W1_COPIERS = ("S", "V", "S")
-W2_COPIER = "V"
+W1_COPIERS = ("S", "V")
+PAIR_COPIERS = ("V", "S")
+W2_COPIER = "S"
 W2_END_COPIERS = ("V", "S")
 
 
@@ -43,10 +43,11 @@ def tile_moe_two_mlp_relu2_kernel(tc, xT, w1, w2, gate, offs, dst, out):
 
     loads = [("x", 0, s) for s in range(PASSES)]
     for e in range(E):
-        loads.extend(("w1", e, s) for s in range(PASSES))
-        if e > 0:
-            loads.insert(len(loads) - (e < LAST), ("w2", e - 1, 0))
-    loads.append(("w2", LAST, 0))
+        loads.extend(("w1", e, s) for s in range(PASSES - 1))
+        if 0 < e < LAST:
+            loads.append(("w2", e - 1, 0))
+        loads.append(("w1", e, PASSES - 1))
+    loads.extend([("w2", LAST - 1, 0), ("w2", LAST, 0)])
     dst_behind = ("w2", 0, 0)
 
     with ExitStack() as ctx:
@@ -110,6 +111,7 @@ def tile_moe_two_mlp_relu2_kernel(tc, xT, w1, w2, gate, offs, dst, out):
             raws[i] = raw[:]
             if i == 0:
                 nc.sync.dma_start(offs_sb[:], offs)
+            if i == 1:
                 nc.sync.dma_start(
                     out=gate_rows[0:GATE_ROWS, :], in_=gate[0:1, :].rearrange("o (r c) -> (o r) c", r=GATE_ROWS)
                 )
@@ -144,7 +146,7 @@ def tile_moe_two_mlp_relu2_kernel(tc, xT, w1, w2, gate, offs, dst, out):
                 for group in range(PACK):
                     sums[group] = last_psum.tile([P, C], F32, name=f"last{group}")
             tiles = [grouped_pool.tile([P, 2 * P * PACK], BF16, name="pair", align_bytes=MX_ALIGN) for u in range(2)]
-            for u, copier in enumerate(("V", "S")):
+            for u, copier in enumerate(PAIR_COPIERS):
                 move(copier, tiles[u][:].rearrange("p (v m j) -> p m j v", v=2, j=PACK), by_pairs(raw)[:, u])
             for u in range(2):
                 chans = slice(2 * u * P, 2 * (u + 1) * P)
@@ -153,7 +155,7 @@ def tile_moe_two_mlp_relu2_kernel(tc, xT, w1, w2, gate, offs, dst, out):
                     if e == LAST:
                         first_layer(e, group, s, sums[group][:], s == 0, s == PASSES - 1)
                     else:
-                        first_layer(e, group, s, sums["bank"][:, group, :], False, group == PACK - 1)
+                        first_layer(e, group, s, sums["bank", e][:, group, :], False, group == PACK - 1)
 
         def quantise(tensor, e, s, first, width, tile):
             if tensor == "x":
@@ -177,7 +179,7 @@ def tile_moe_two_mlp_relu2_kernel(tc, xT, w1, w2, gate, offs, dst, out):
                 gather(slot_codes[s], x_codes[s], first, end)
                 gather(slot_scales, x_scales, first, end)
 
-        def first_layer(e, group, s, into, first, last):
+        def first_layer(e, group, s, into, start, stop):
             codes, scales = weights["w1", e, s]
             chans = slice(group * P, (group + 1) * P)
             slots = slice(e * C, (e + 1) * C)
@@ -187,23 +189,18 @@ def tile_moe_two_mlp_relu2_kernel(tc, xT, w1, w2, gate, offs, dst, out):
                 lhsT_scale=scales[:, chans],
                 rhs=slot_codes[s][:, slots].bitcast(FP8X4),
                 rhs_scale=slot_scales[4 * s : P, slots],
-                start=first,
-                stop=last,
+                start=start,
+                stop=stop,
             )
 
         def first_layer_pass(e, s):
             if s == 0:
-                sums["bank"] = sum_psum.tile([P, PACK, C], F32, name="bank")
+                sums["bank", e] = sum_psum.tile([P, PACK, C], F32, name="bank")
             for group in range(PACK):
-                first, last = (s, group) == (0, 0), (s, group) == (PASSES - 1, PACK - 1)
-                first_layer(e, group, s, sums["bank"][:, group, :], first, last)
+                first_layer(e, group, s, sums["bank", e][:, group, :], (s, group) == (0, 0), False)
 
-        def bank_relu(bank, spent=None):
-            if spent is None:
-                relu = relu_pool.tile([P, C, PACK], F32, name="relu")[:]
-            else:
-                relu = spent[:, 0, :].rearrange("p (c t) -> p c t", t=PACK)
-            nc.scalar.activation(relu, bank[:].rearrange("p t c -> p c t"), RELU)
+        def bank_relu(e, relu):
+            nc.scalar.activation(relu, sums["bank", e][:].rearrange("p t c -> p c t"), RELU)
             return relu
 
         def last_relu():
@@ -240,14 +237,8 @@ def tile_moe_two_mlp_relu2_kernel(tc, xT, w1, w2, gate, offs, dst, out):
                 )
             return y
 
-        def scatter(e, halves, y, spent=None):
-            if spent is not None:
-                y_sb = spent[:, 0, 0 : len(halves) * C].rearrange("p (n c) -> p n c", c=C)
-            elif (e, halves[0]) == (LAST - 1, 1):
-                y_sb = relu_pool.tile([P, len(halves), C], F32, name="relu")
-            else:
-                y_sb = small_pool.tile([P, len(halves), C], F32, name=f"y_sb{halves[0]}")
-            nc.scalar.copy(out=y_sb[:, :, :], in_=y[:])
+        def scatter(e, halves, y, y_sb):
+            nc.scalar.copy(out=y_sb, in_=y[:])
             listed = dst_sb[:, e * C // LIST_ROWS : (e + 1) * C // LIST_ROWS]
             for n, half in enumerate(halves):
                 nc.vector.tensor_tensor(
@@ -262,7 +253,7 @@ def tile_moe_two_mlp_relu2_kernel(tc, xT, w1, w2, gate, offs, dst, out):
             if i + AHEAD < len(loads):
                 load(i + AHEAD)
             raw = raws.pop(i)
-            if (tensor, s) == ("x", 1):
+            if (tensor, s) == ("x", 2):
                 spread_gate()
             if tensor == "x":
                 tiles = [interleave(raw, n * WIDTH, WIDTH, copier, "grouped") for n, copier in enumerate(X_COPIERS)]
@@ -270,21 +261,28 @@ def tile_moe_two_mlp_relu2_kernel(tc, xT, w1, w2, gate, offs, dst, out):
                     quantise(tensor, e, s, n * WIDTH, WIDTH, tile)
                 gather_pass(s)
             elif tensor == "w1":
-                if e == LAST or (e >= LAST - 2 and s == PASSES - 1):
+                if e == LAST or s == PASSES - 1:
                     shared_pass(e, s, raw)
                 else:
                     quantise(tensor, e, s, 0, H, interleave_w1(raw, W1_COPIERS[s]))
                     first_layer_pass(e, s)
+                spent = raw[:, 0, :]
+                if s == 0 and 0 < e < LAST:
+                    square_and_quantise(e - 1, bank_relu(e - 1, spent.rearrange("p (c t) -> p c t", t=PACK)))
                 if s == PASSES - 1 and 0 < e < LAST:
-                    scatter(e - 1, range(HALVES), waiting, raw)
-                if s == 0 and e in HELD:
-                    square_and_quantise(e - 1, bank_relu(full, raw))
-                if s == PASSES - 1 and e + 1 in HELD:
-                    full = sums["bank"]
-                elif s == PASSES - 1:
-                    square_and_quantise(e, last_relu() if e == LAST else bank_relu(sums["bank"]))
+                    y_sb = spent[:, 0 : HALVES * C].rearrange("p (n c) -> p n c", c=C)
+                    scatter(e - 1, range(HALVES), products_waiting, y_sb)
+                if (e, s) == (LAST - 1, PASSES - 1):
+                    square_and_quantise(e, bank_relu(e, relu_pool.tile([P, C, PACK], F32, name="relu")[:]))
+                if (e, s) == (LAST, PASSES - 1):
+                    square_and_quantise(e, last_relu())
             elif e < LAST - 1:
-                waiting = products(e, raw, range(HALVES), "S" if e == LAST - 2 else W2_COPIER)
+                products_waiting = products(e, raw, range(HALVES), W2_COPIER)
             else:
                 for half, copier in enumerate(W2_END_COPIERS):
-                    scatter(e, [half], products(e, raw, [half], copier))
+                    y = products(e, raw, [half], copier)
+                    if (e, half) == (LAST - 1, 1):
+                        y_sb = relu_pool.tile([P, 1, C], F32, name="relu")
+                    else:
+                        y_sb = small_pool.tile([P, 1, C], F32, name=f"y_sb{half}")
+                    scatter(e, [half], y, y_sb[:])

@@ -13,6 +13,7 @@ U16 = mybir.dt.uint16
 U8 = mybir.dt.uint8
 FP8X4 = mybir.dt.float8_e4m3fn_x4
 RELU = mybir.ActivationFunctionType.Relu
+COPY = mybir.ActivationFunctionType.Copy
 SQUARE = mybir.ActivationFunctionType.Square
 MULT = mybir.AluOpType.mult
 
@@ -35,7 +36,6 @@ X_COPIERS = ("V", "S")
 W1_COPIERS = ("S", "V")
 PAIR_COPIERS = ("V", "S")
 W2_COPIER = "S"
-W2_END_COPIERS = ("V", "S")
 
 
 def tile_moe_two_mlp_relu2_kernel(tc, xT, w1, w2, gate, offs, dst, out):
@@ -107,7 +107,15 @@ def tile_moe_two_mlp_relu2_kernel(tc, xT, w1, w2, gate, offs, dst, out):
             else:
                 raw = raw2_pool.tile([P, PACK, N], F32, name="raw2", align_bytes=DMA_ALIGN)
                 src = w2[e]
-            nc.sync.dma_start(out=raw[:], in_=src.rearrange("(p j) c -> p j c", j=PACK))
+            src = src.rearrange("(p j) c -> p j c", j=PACK)
+            if loads[i] == ("w1", LAST, PASSES - 1):
+                other = raw_pool.tile([P, PACK, H // 2], F32, name="raw", align_bytes=DMA_ALIGN)
+                first = raw[:].rearrange("p j c -> p (j c)")[:, 0 : PACK * H // 2].rearrange("p (j c) -> p j c", j=PACK)
+                nc.sync.dma_start(out=first, in_=src[:, :, 0 : H // 2])
+                nc.sync.dma_start(out=other[:], in_=src[:, :, H // 2 : H])
+                raws[i] = (first, other[:])
+                return
+            nc.sync.dma_start(out=raw[:], in_=src)
             raws[i] = raw[:]
             if i == 0:
                 nc.sync.dma_start(offs_sb[:], offs)
@@ -124,8 +132,8 @@ def tile_moe_two_mlp_relu2_kernel(tc, xT, w1, w2, gate, offs, dst, out):
             else:
                 nc.vector.tensor_copy(out=dest, in_=src)
 
-        def interleave(raw, first, width, copier, tag):
-            tile = grouped_pool.tile([P, width * PACK], BF16, name=tag, align_bytes=MX_ALIGN)
+        def interleave(raw, first, width, copier, tag, dest=None):
+            tile = dest if dest is not None else grouped_pool.tile([P, width * PACK], BF16, name=tag, align_bytes=MX_ALIGN)
             src = raw[:, :, first : first + width].rearrange("p j (c i) -> p c j i", i=4)
             move(copier, tile[:].rearrange("p (c i j) -> p c j i", i=4, j=PACK), src)
             return tile
@@ -146,8 +154,12 @@ def tile_moe_two_mlp_relu2_kernel(tc, xT, w1, w2, gate, offs, dst, out):
                 for group in range(PACK):
                     sums[group] = last_psum.tile([P, C], F32, name=f"last{group}")
             tiles = [grouped_pool.tile([P, 2 * P * PACK], BF16, name="pair", align_bytes=MX_ALIGN) for u in range(2)]
-            for u, copier in enumerate(PAIR_COPIERS):
-                move(copier, tiles[u][:].rearrange("p (v m j) -> p m j v", v=2, j=PACK), by_pairs(raw)[:, u])
+            parts = raw if isinstance(raw, tuple) else (raw,)
+            for n, part in enumerate(parts):
+                ms = slice(n * P // len(parts), (n + 1) * P // len(parts))
+                for u, copier in enumerate(PAIR_COPIERS):
+                    dest = tiles[u][:].rearrange("p (v m j) -> p m j v", v=2, j=PACK)
+                    move(copier, dest[:, ms], by_pairs(part)[:, u])
             for u in range(2):
                 chans = slice(2 * u * P, 2 * (u + 1) * P)
                 nc.vector.quantize_mx(out=codes[:, chans].bitcast(FP8X4), scales=scales[:, chans], in_=tiles[u][:])
@@ -203,17 +215,25 @@ def tile_moe_two_mlp_relu2_kernel(tc, xT, w1, w2, gate, offs, dst, out):
             nc.scalar.activation(relu, sums["bank", e][:].rearrange("p t c -> p c t"), RELU)
             return relu
 
-        def last_relu():
-            relu = relu_pool.tile([P, PACK, C], F32, name="relu")
+        def last_relu(relu):
             for group in range(PACK):
                 nc.scalar.activation(relu[:, group, :], sums[group][:], RELU)
-            return relu[:].rearrange("p t c -> p c t")
+            return relu.rearrange("p t c -> p c t")
 
         def square_and_quantise(e, relu):
-            tile = small_pool.tile([P, C * PACK], BF16, name="h", align_bytes=MX_ALIGN)
+            if e == LAST:
+                tile = relu_pool.tile([P, C * PACK], BF16, name="h_last", align_bytes=MX_ALIGN)
+            else:
+                tile = small_pool.tile([P, C * PACK], BF16, name="h", align_bytes=MX_ALIGN)
             h = tile[:].rearrange("p (c t) -> p c t", t=PACK)
             nc.scalar.activation(h, relu, SQUARE)
-            codes = small_pool.tile([P, C], U32, name="h_codes", align_bytes=MX_ALIGN)
+            if e == LAST:
+                return tile
+            quantise_h(e, tile)
+
+        def quantise_h(e, tile, codes=None):
+            if codes is None:
+                codes = small_pool.tile([P, C], U32, name="h_codes", align_bytes=MX_ALIGN)
             scales = small_pool.tile([P, C], U8, name="h_scales", align_bytes=MX_ALIGN)
             nc.vector.quantize_mx(out=codes[:].bitcast(FP8X4), scales=scales[:], in_=tile[:])
             hidden[e] = (codes, scales)
@@ -244,8 +264,6 @@ def tile_moe_two_mlp_relu2_kernel(tc, xT, w1, w2, gate, offs, dst, out):
                 nc.vector.tensor_tensor(
                     out_sb[half][:].indirect(listed), y_sb[:, n, :], gate_sb[:, e * C : (e + 1) * C], MULT
                 )
-                if e == LAST:
-                    nc.sync.dma_start(out=out[half * P : (half + 1) * P, :], in_=out_sb[half][:])
 
         for i in range(AHEAD):
             load(i)
@@ -266,23 +284,73 @@ def tile_moe_two_mlp_relu2_kernel(tc, xT, w1, w2, gate, offs, dst, out):
                 else:
                     quantise(tensor, e, s, 0, H, interleave_w1(raw, W1_COPIERS[s]))
                     first_layer_pass(e, s)
-                spent = raw[:, 0, :]
+                spent = raw[:, 0, :] if e < LAST else None
                 if s == 0 and 0 < e < LAST:
                     square_and_quantise(e - 1, bank_relu(e - 1, spent.rearrange("p (c t) -> p c t", t=PACK)))
                 if s == PASSES - 1 and 0 < e < LAST:
                     y_sb = spent[:, 0 : HALVES * C].rearrange("p (n c) -> p n c", c=C)
                     scatter(e - 1, range(HALVES), products_waiting, y_sb)
                 if (e, s) == (LAST - 1, PASSES - 1):
-                    square_and_quantise(e, bank_relu(e, relu_pool.tile([P, C, PACK], F32, name="relu")[:]))
-                if (e, s) == (LAST, PASSES - 1):
-                    square_and_quantise(e, last_relu())
+                    square_and_quantise(e, bank_relu(e, relu_pool.tile([P, C, PACK], F32, name="relu", align_bytes=MX_ALIGN)[:]))
             elif e < LAST - 1:
                 products_waiting = products(e, raw, range(HALVES), W2_COPIER)
             else:
-                for half, copier in enumerate(W2_END_COPIERS):
-                    y = products(e, raw, [half], copier)
-                    if (e, half) == (LAST - 1, 1):
-                        y_sb = relu_pool.tile([P, 1, C], F32, name="relu")
-                    else:
-                        y_sb = small_pool.tile([P, 1, C], F32, name=f"y_sb{half}")
-                    scatter(e, [half], y, y_sb[:])
+                raws[tensor, e] = raw
+
+        def product(e, codes, scales, y):
+            h_codes, h_scales = hidden[e]
+            nc.tensor.matmul_mx(
+                out=y[:],
+                lhsT=codes.bitcast(FP8X4),
+                lhsT_scale=scales,
+                rhs=h_codes[:].bitcast(FP8X4),
+                rhs_scale=h_scales[:],
+                start=True,
+                stop=True,
+            )
+            return y
+
+        def places(e, half):
+            return out_sb[half][:].indirect(dst_sb[:, e * C // LIST_ROWS : (e + 1) * C // LIST_ROWS])
+
+        def gated(e, y, tile=None):
+            if tile is None:
+                tile = grouped_pool.tile([P, C], F32, name="gated")
+            nc.vector.tensor_tensor(tile[:], y[:], gate_sb[:, e * C : (e + 1) * C], MULT)
+            return tile
+
+        def store(half):
+            nc.sync.dma_start(out=out[half * P : (half + 1) * P, :], in_=out_sb[half][:])
+
+        def scatter_gated(engine, e, half, tile):
+            if engine == "S":
+                nc.scalar.activation(places(e, half), tile[:], COPY)
+            else:
+                nc.vector.tensor_copy(places(e, half), tile[:])
+
+        a, b = LAST - 1, LAST
+        a0 = interleave(raws["w2", a], 0, P, "S", "grouped2")
+        h_last = square_and_quantise(b, last_relu(raws["w2", a][:, :, 0:P]))
+        a1 = interleave(raws["w2", a], P, P, "V", "grouped2")
+        quantise("w2", a, 0, 0, P, a0)
+        ya0 = product(a, *weights["w2", a, 0], y_psum.tile([P, C], F32, name="y0"))
+        quantise("w2", a, 0, P, P, a1)
+        ya1 = product(a, *weights["w2", a, 0], y_psum.tile([P, C], F32, name="y1"))
+        b0 = relu_pool.tile([P, P * PACK], BF16, name="b0", align_bytes=MX_ALIGN)
+        interleave(raws["w2", b], 0, P, "V", "", b0)
+        b1 = interleave(raws["w2", b], P, P, "V", "grouped2")
+        quantise("w2", b, 0, 0, P, b0)
+        ga0 = gated(a, ya0, raws["w2", b][:, 0, 0:P])
+        scatter_gated("S", a, 0, ga0)
+        quantise_h(b, h_last, relu_pool.tile([P, C], U32, name="b0", align_bytes=MX_ALIGN))
+        yb0 = product(b, *weights["w2", b, 0], sum_psum.tile([P, C], F32, name="bank"))
+        quantise("w2", b, 0, P, P, b1)
+        yb1 = product(b, *weights["w2", b, 0], sum_psum.tile([P, C], F32, name="bank"))
+        ga1 = gated(a, ya1, raws["w2", b][:, 1, 0:P])
+        scatter_gated("S", a, 1, ga1)
+        gb0 = gated(b, yb0)
+        gb1 = gated(b, yb1)
+        scatter_gated("V", b, 0, gb0)
+        store(0)
+        scatter_gated("S", b, 1, gb1)
+        store(1)

@@ -47,14 +47,14 @@ def tile_moe_two_mlp_relu2_kernel(tc, xT, w1, w2, gate, offs, dst, out):
         if 0 < e < LAST:
             loads.append(("w2", e - 1, 0))
         loads.append(("w1", e, PASSES - 1))
-    loads.extend([("w2", LAST - 1, 0), ("w2", LAST, 0)])
+    loads.extend(("half", e, half) for half in range(HALVES) for e in (LAST - 1, LAST))
     dst_behind = ("w2", 0, 0)
 
     with ExitStack() as ctx:
         keep = ctx.enter_context(tc.tile_pool(name="keep", bufs=1))
         raw_pool = ctx.enter_context(tc.tile_pool(name="raw", bufs=8))
         rawx_pool = ctx.enter_context(tc.tile_pool(name="rawx", bufs=PASSES))
-        raw2_pool = ctx.enter_context(tc.tile_pool(name="raw2", bufs=3))
+        raw2_pool = ctx.enter_context(tc.tile_pool(name="raw2", bufs=2))
         grouped_pool = ctx.enter_context(tc.tile_pool(name="grouped", bufs=4))
         code_pool = ctx.enter_context(tc.tile_pool(name="codes", bufs=PASSES + 1))
         small_pool = ctx.enter_context(tc.tile_pool(name="small", bufs=3))
@@ -104,6 +104,9 @@ def tile_moe_two_mlp_relu2_kernel(tc, xT, w1, w2, gate, offs, dst, out):
             elif tensor == "w1":
                 raw = raw_pool.tile([P, PACK, H], F32, name="raw", align_bytes=DMA_ALIGN)
                 src = w1[e, s * PASS : (s + 1) * PASS, :]
+            elif tensor == "half":
+                raw = keep.tile([P, PACK, P], F32, name=f"half{e}{s}", align_bytes=DMA_ALIGN)
+                src = w2[e, :, s * P : (s + 1) * P]
             else:
                 raw = raw2_pool.tile([P, PACK, N], F32, name="raw2", align_bytes=DMA_ALIGN)
                 src = w2[e]
@@ -161,9 +164,15 @@ def tile_moe_two_mlp_relu2_kernel(tc, xT, w1, w2, gate, offs, dst, out):
                     dest = tiles[u][:].rearrange("p (v m j) -> p m j v", v=2, j=PACK)
                     move(copier, dest[:, ms], by_pairs(part)[:, u])
             for u in range(2):
-                chans = slice(2 * u * P, 2 * (u + 1) * P)
-                nc.vector.quantize_mx(out=codes[:, chans].bitcast(FP8X4), scales=scales[:, chans], in_=tiles[u][:])
+                singly = (e, s, u) == (LAST, PASSES - 1, 1)
+                if not singly:
+                    chans = slice(2 * u * P, 2 * (u + 1) * P)
+                    nc.vector.quantize_mx(out=codes[:, chans].bitcast(FP8X4), scales=scales[:, chans], in_=tiles[u][:])
                 for group in (2 * u, 2 * u + 1):
+                    if singly:
+                        chans = slice(group * P, (group + 1) * P)
+                        part = tiles[u][:, group % 2 * PASS : (group % 2 + 1) * PASS]
+                        nc.vector.quantize_mx(out=codes[:, chans].bitcast(FP8X4), scales=scales[:, chans], in_=part)
                     if e == LAST:
                         first_layer(e, group, s, sums[group][:], s == 0, s == PASSES - 1)
                     else:
@@ -292,10 +301,10 @@ def tile_moe_two_mlp_relu2_kernel(tc, xT, w1, w2, gate, offs, dst, out):
                     scatter(e - 1, range(HALVES), products_waiting, y_sb)
                 if (e, s) == (LAST - 1, PASSES - 1):
                     square_and_quantise(e, bank_relu(e, relu_pool.tile([P, C, PACK], F32, name="relu", align_bytes=MX_ALIGN)[:]))
-            elif e < LAST - 1:
+            elif tensor == "w2":
                 products_waiting = products(e, raw, range(HALVES), W2_COPIER)
             else:
-                raws[tensor, e] = raw
+                raws[e, s] = raw
 
         def product(e, codes, scales, y):
             h_codes, h_scales = hidden[e]
@@ -329,24 +338,24 @@ def tile_moe_two_mlp_relu2_kernel(tc, xT, w1, w2, gate, offs, dst, out):
                 nc.vector.tensor_copy(places(e, half), tile[:])
 
         a, b = LAST - 1, LAST
-        a0 = interleave(raws["w2", a], 0, P, "S", "grouped2")
-        h_last = square_and_quantise(b, last_relu(raws["w2", a][:, :, 0:P]))
-        a1 = interleave(raws["w2", a], P, P, "V", "grouped2")
+        a0 = interleave(raws[a, 0], 0, P, "S", "grouped2")
+        h_last = square_and_quantise(b, last_relu(raws[a, 0]))
+        b0 = interleave(raws[b, 0], 0, P, "V", "grouped2")
         quantise("w2", a, 0, 0, P, a0)
         ya0 = product(a, *weights["w2", a, 0], y_psum.tile([P, C], F32, name="y0"))
+        quantise("w2", b, 0, 0, P, b0)
+        first = weights["w2", b, 0]
+        a1 = interleave(raws[a, 1], 0, P, "V", "grouped2")
         quantise("w2", a, 0, P, P, a1)
         ya1 = product(a, *weights["w2", a, 0], y_psum.tile([P, C], F32, name="y1"))
-        b0 = relu_pool.tile([P, P * PACK], BF16, name="b0", align_bytes=MX_ALIGN)
-        interleave(raws["w2", b], 0, P, "V", "", b0)
-        b1 = interleave(raws["w2", b], P, P, "V", "grouped2")
-        quantise("w2", b, 0, 0, P, b0)
-        ga0 = gated(a, ya0, raws["w2", b][:, 0, 0:P])
+        ga0 = gated(a, ya0, raws[a, 1][:, 0, :])
         scatter_gated("S", a, 0, ga0)
-        quantise_h(b, h_last, relu_pool.tile([P, C], U32, name="b0", align_bytes=MX_ALIGN))
-        yb0 = product(b, *weights["w2", b, 0], sum_psum.tile([P, C], F32, name="bank"))
+        b1 = interleave(raws[b, 1], 0, P, "V", "grouped2")
+        quantise_h(b, h_last)
+        yb0 = product(b, *first, sum_psum.tile([P, C], F32, name="bank"))
         quantise("w2", b, 0, P, P, b1)
         yb1 = product(b, *weights["w2", b, 0], sum_psum.tile([P, C], F32, name="bank"))
-        ga1 = gated(a, ya1, raws["w2", b][:, 1, 0:P])
+        ga1 = gated(a, ya1, relu_pool.tile([P, C], F32, name="h_last", align_bytes=MX_ALIGN))
         scatter_gated("S", a, 1, ga1)
         gb0 = gated(b, yb0)
         gb1 = gated(b, yb1)

@@ -24,7 +24,7 @@ PASSES = K // PASS
 SLOTS = E * C
 HALVES = N // P
 LAST = E - 1
-WIDTH = 512
+WIDTH = T // 2
 AHEAD = 6
 GATE_ROWS = 2
 GATE_BLOCKS = E // GATE_ROWS
@@ -48,6 +48,7 @@ def tile_moe_two_mlp_relu2_kernel(tc, xT, w1, w2, gate, offs, dst, out):
             loads.append(("w2", e - 1, 0))
         loads.append(("w1", e, PASSES - 1))
     loads.extend(("half", e, half) for half in range(HALVES) for e in (LAST - 1, LAST))
+    last_pass = ("w1", LAST, PASSES - 1)
     dst_behind = ("w2", 0, 0)
 
     with ExitStack() as ctx:
@@ -58,7 +59,7 @@ def tile_moe_two_mlp_relu2_kernel(tc, xT, w1, w2, gate, offs, dst, out):
         grouped_pool = ctx.enter_context(tc.tile_pool(name="grouped", bufs=4))
         code_pool = ctx.enter_context(tc.tile_pool(name="codes", bufs=PASSES + 1))
         small_pool = ctx.enter_context(tc.tile_pool(name="small", bufs=3))
-        relu_pool = ctx.enter_context(tc.tile_pool(name="relu", bufs=1))
+        end_pool = ctx.enter_context(tc.tile_pool(name="relu", bufs=1))
         sum_psum = ctx.enter_context(tc.psum_pool(name="sum_psum", bufs=2))
         last_psum = ctx.enter_context(tc.psum_pool(name="last_psum", bufs=1))
         y_psum = ctx.enter_context(tc.psum_pool(name="y_psum", bufs=1))
@@ -94,7 +95,7 @@ def tile_moe_two_mlp_relu2_kernel(tc, xT, w1, w2, gate, offs, dst, out):
                 width = GATE_BLOCKS * C
                 nc.scalar.copy(out=gate_sb[:, r * width : (r + 1) * width], in_=spread[:].rearrange("p b c -> p (b c)"))
 
-        raws, weights, hidden, sums = {}, {}, {}, {}
+        raws, halves, weights, hidden, sums = {}, {}, {}, {}, {}
 
         def load(i):
             tensor, e, s = loads[i]
@@ -111,12 +112,12 @@ def tile_moe_two_mlp_relu2_kernel(tc, xT, w1, w2, gate, offs, dst, out):
                 raw = raw2_pool.tile([P, PACK, N], F32, name="raw2", align_bytes=DMA_ALIGN)
                 src = w2[e]
             src = src.rearrange("(p j) c -> p j c", j=PACK)
-            if loads[i] == ("w1", LAST, PASSES - 1):
-                other = raw_pool.tile([P, PACK, H // 2], F32, name="raw", align_bytes=DMA_ALIGN)
-                first = raw[:].rearrange("p j c -> p (j c)")[:, 0 : PACK * H // 2].rearrange("p (j c) -> p j c", j=PACK)
-                nc.sync.dma_start(out=first, in_=src[:, :, 0 : H // 2])
-                nc.sync.dma_start(out=other[:], in_=src[:, :, H // 2 : H])
-                raws[i] = (first, other[:])
+            if loads[i] == last_pass:
+                right = raw_pool.tile([P, PACK, H // 2], F32, name="raw", align_bytes=DMA_ALIGN)
+                left = raw[:].rearrange("p j c -> p (j c)")[:, 0 : PACK * H // 2].rearrange("p (j c) -> p j c", j=PACK)
+                nc.sync.dma_start(out=left, in_=src[:, :, 0 : H // 2])
+                nc.sync.dma_start(out=right[:], in_=src[:, :, H // 2 : H])
+                raws[i] = (left, right[:])
                 return
             nc.sync.dma_start(out=raw[:], in_=src)
             raws[i] = raw[:]
@@ -135,8 +136,8 @@ def tile_moe_two_mlp_relu2_kernel(tc, xT, w1, w2, gate, offs, dst, out):
             else:
                 nc.vector.tensor_copy(out=dest, in_=src)
 
-        def interleave(raw, first, width, copier, tag, dest=None):
-            tile = dest if dest is not None else grouped_pool.tile([P, width * PACK], BF16, name=tag, align_bytes=MX_ALIGN)
+        def interleave(raw, first, width, copier, tag):
+            tile = grouped_pool.tile([P, width * PACK], BF16, name=tag, align_bytes=MX_ALIGN)
             src = raw[:, :, first : first + width].rearrange("p j (c i) -> p c j i", i=4)
             move(copier, tile[:].rearrange("p (c i j) -> p c j i", i=4, j=PACK), src)
             return tile
@@ -149,7 +150,7 @@ def tile_moe_two_mlp_relu2_kernel(tc, xT, w1, w2, gate, offs, dst, out):
             move(copier, tile[:].rearrange("p (u v m j) -> p u m j v", u=2, v=2, j=PACK), by_pairs(raw))
             return tile
 
-        def shared_pass(e, s, raw):
+        def shared_pass(e, s, parts):
             codes = code_pool.tile([P, H], U32, name="codes_w1", align_bytes=MX_ALIGN)[:, :]
             scales = code_pool.tile([P, H], U8, name="scales_w1", align_bytes=MX_ALIGN)[:, :]
             weights["w1", e, s] = (codes, scales)
@@ -157,26 +158,24 @@ def tile_moe_two_mlp_relu2_kernel(tc, xT, w1, w2, gate, offs, dst, out):
                 for group in range(PACK):
                     sums[group] = last_psum.tile([P, C], F32, name=f"last{group}")
             tiles = [grouped_pool.tile([P, 2 * P * PACK], BF16, name="pair", align_bytes=MX_ALIGN) for u in range(2)]
-            parts = raw if isinstance(raw, tuple) else (raw,)
             for n, part in enumerate(parts):
-                ms = slice(n * P // len(parts), (n + 1) * P // len(parts))
+                columns = slice(n * P // len(parts), (n + 1) * P // len(parts))
                 for u, copier in enumerate(PAIR_COPIERS):
                     dest = tiles[u][:].rearrange("p (v m j) -> p m j v", v=2, j=PACK)
-                    move(copier, dest[:, ms], by_pairs(part)[:, u])
-            for u in range(2):
-                singly = (e, s, u) == (LAST, PASSES - 1, 1)
-                if not singly:
-                    chans = slice(2 * u * P, 2 * (u + 1) * P)
-                    nc.vector.quantize_mx(out=codes[:, chans].bitcast(FP8X4), scales=scales[:, chans], in_=tiles[u][:])
-                for group in (2 * u, 2 * u + 1):
-                    if singly:
-                        chans = slice(group * P, (group + 1) * P)
-                        part = tiles[u][:, group % 2 * PASS : (group % 2 + 1) * PASS]
-                        nc.vector.quantize_mx(out=codes[:, chans].bitcast(FP8X4), scales=scales[:, chans], in_=part)
-                    if e == LAST:
-                        first_layer(e, group, s, sums[group][:], s == 0, s == PASSES - 1)
-                    else:
+                    move(copier, dest[:, columns], by_pairs(part)[:, u])
+            together = 1 if ("w1", e, s) == last_pass else 2
+            for first in range(0, PACK, together):
+                chans = slice(first * P, (first + together) * P)
+                values = tiles[first // 2][:, first % 2 * PASS : (first % 2 + together) * PASS]
+                nc.vector.quantize_mx(out=codes[:, chans].bitcast(FP8X4), scales=scales[:, chans], in_=values)
+                for group in range(first, first + together):
+                    if e < LAST:
                         first_layer(e, group, s, sums["bank", e][:, group, :], False, group == PACK - 1)
+                    elif s == 1:
+                        first_layer(e, group, 1, sums[group][:], True, False)
+                        first_layer(e, group, 0, sums[group][:], False, False)
+                    elif s == PASSES - 1:
+                        first_layer(e, group, s, sums[group][:], False, True)
 
         def quantise(tensor, e, s, first, width, tile):
             if tensor == "x":
@@ -229,50 +228,62 @@ def tile_moe_two_mlp_relu2_kernel(tc, xT, w1, w2, gate, offs, dst, out):
                 nc.scalar.activation(relu[:, group, :], sums[group][:], RELU)
             return relu.rearrange("p t c -> p c t")
 
-        def square_and_quantise(e, relu):
-            if e == LAST:
-                tile = relu_pool.tile([P, C * PACK], BF16, name="h_last", align_bytes=MX_ALIGN)
-            else:
-                tile = small_pool.tile([P, C * PACK], BF16, name="h", align_bytes=MX_ALIGN)
-            h = tile[:].rearrange("p (c t) -> p c t", t=PACK)
-            nc.scalar.activation(h, relu, SQUARE)
-            if e == LAST:
-                return tile
-            quantise_h(e, tile)
+        def square(relu, tile):
+            nc.scalar.activation(tile[:].rearrange("p (c t) -> p c t", t=PACK), relu, SQUARE)
+            return tile
 
-        def quantise_h(e, tile, codes=None):
-            if codes is None:
-                codes = small_pool.tile([P, C], U32, name="h_codes", align_bytes=MX_ALIGN)
+        def quantise_h(e, tile):
+            codes = small_pool.tile([P, C], U32, name="h_codes", align_bytes=MX_ALIGN)
             scales = small_pool.tile([P, C], U8, name="h_scales", align_bytes=MX_ALIGN)
             nc.vector.quantize_mx(out=codes[:].bitcast(FP8X4), scales=scales[:], in_=tile[:])
             hidden[e] = (codes, scales)
 
-        def products(e, raw, halves, copier):
-            first, width = halves[0] * P, len(halves) * P
-            quantise("w2", e, 0, first, width, interleave(raw, first, width, copier, "grouped2"))
-            w_codes, w_scales = weights["w2", e, 0]
+        def square_and_quantise(e, relu):
+            quantise_h(e, square(relu, small_pool.tile([P, C * PACK], BF16, name="h", align_bytes=MX_ALIGN)))
+
+        def second_layer(e, codes, scales, into):
             h_codes, h_scales = hidden[e]
-            y = y_psum.tile([P, len(halves), C], F32, name=f"y{halves[0]}")
-            for n in range(len(halves)):
-                chans = slice(n * P, (n + 1) * P)
-                nc.tensor.matmul_mx(
-                    out=y[:, n, :],
-                    lhsT=w_codes[:, chans].bitcast(FP8X4),
-                    lhsT_scale=w_scales[:, chans],
-                    rhs=h_codes[:].bitcast(FP8X4),
-                    rhs_scale=h_scales[:],
-                    start=True,
-                    stop=True,
-                )
+            nc.tensor.matmul_mx(
+                out=into,
+                lhsT=codes.bitcast(FP8X4),
+                lhsT_scale=scales,
+                rhs=h_codes[:].bitcast(FP8X4),
+                rhs_scale=h_scales[:],
+                start=True,
+                stop=True,
+            )
+            return into
+
+        def products(e, raw):
+            quantise("w2", e, 0, 0, N, interleave(raw, 0, N, W2_COPIER, "grouped2"))
+            codes, scales = weights["w2", e, 0]
+            y = y_psum.tile([P, HALVES, C], F32, name="y0")
+            for half in range(HALVES):
+                chans = slice(half * P, (half + 1) * P)
+                second_layer(e, codes[:, chans], scales[:, chans], y[:, half, :])
             return y
 
-        def scatter(e, halves, y, y_sb):
+        def places(e, half):
+            return out_sb[half][:].indirect(dst_sb[:, e * C // LIST_ROWS : (e + 1) * C // LIST_ROWS])
+
+        def gates(e):
+            return gate_sb[:, e * C : (e + 1) * C]
+
+        def scatter_times_gate(e, y, y_sb):
             nc.scalar.copy(out=y_sb, in_=y[:])
-            listed = dst_sb[:, e * C // LIST_ROWS : (e + 1) * C // LIST_ROWS]
-            for n, half in enumerate(halves):
-                nc.vector.tensor_tensor(
-                    out_sb[half][:].indirect(listed), y_sb[:, n, :], gate_sb[:, e * C : (e + 1) * C], MULT
-                )
+            for half in range(HALVES):
+                nc.vector.tensor_tensor(places(e, half), y_sb[:, half, :], gates(e), MULT)
+
+        def half_codes(e, half, tile):
+            quantise("w2", e, half, 0, P, tile)
+            return weights["w2", e, half]
+
+        def gated(e, y, into):
+            nc.vector.tensor_tensor(into, y, gates(e), MULT)
+            return into
+
+        def store(half):
+            nc.sync.dma_start(out=out[half * P : (half + 1) * P, :], in_=out_sb[half][:])
 
         for i in range(AHEAD):
             load(i)
@@ -288,78 +299,51 @@ def tile_moe_two_mlp_relu2_kernel(tc, xT, w1, w2, gate, offs, dst, out):
                     quantise(tensor, e, s, n * WIDTH, WIDTH, tile)
                 gather_pass(s)
             elif tensor == "w1":
-                if e == LAST or s == PASSES - 1:
+                if loads[i] == last_pass:
                     shared_pass(e, s, raw)
+                elif e == LAST or s == PASSES - 1:
+                    shared_pass(e, s, (raw,))
                 else:
                     quantise(tensor, e, s, 0, H, interleave_w1(raw, W1_COPIERS[s]))
                     first_layer_pass(e, s)
-                spent = raw[:, 0, :] if e < LAST else None
                 if s == 0 and 0 < e < LAST:
-                    square_and_quantise(e - 1, bank_relu(e - 1, spent.rearrange("p (c t) -> p c t", t=PACK)))
+                    spent = raw[:, 0, :].rearrange("p (c t) -> p c t", t=PACK)
+                    square_and_quantise(e - 1, bank_relu(e - 1, spent))
                 if s == PASSES - 1 and 0 < e < LAST:
-                    y_sb = spent[:, 0 : HALVES * C].rearrange("p (n c) -> p n c", c=C)
-                    scatter(e - 1, range(HALVES), products_waiting, y_sb)
+                    spent = raw[:, 0, 0 : HALVES * C].rearrange("p (n c) -> p n c", c=C)
+                    scatter_times_gate(e - 1, products_waiting, spent)
                 if (e, s) == (LAST - 1, PASSES - 1):
-                    square_and_quantise(e, bank_relu(e, relu_pool.tile([P, C, PACK], F32, name="relu", align_bytes=MX_ALIGN)[:]))
+                    relu = end_pool.tile([P, C, PACK], F32, name="relu", align_bytes=MX_ALIGN)
+                    square_and_quantise(e, bank_relu(e, relu[:]))
             elif tensor == "w2":
-                products_waiting = products(e, raw, range(HALVES), W2_COPIER)
+                products_waiting = products(e, raw)
             else:
-                raws[e, s] = raw
+                halves[e, s] = raw
 
-        def product(e, codes, scales, y):
-            h_codes, h_scales = hidden[e]
-            nc.tensor.matmul_mx(
-                out=y[:],
-                lhsT=codes.bitcast(FP8X4),
-                lhsT_scale=scales,
-                rhs=h_codes[:].bitcast(FP8X4),
-                rhs_scale=h_scales[:],
-                start=True,
-                stop=True,
-            )
-            return y
-
-        def places(e, half):
-            return out_sb[half][:].indirect(dst_sb[:, e * C // LIST_ROWS : (e + 1) * C // LIST_ROWS])
-
-        def gated(e, y, tile=None):
-            if tile is None:
-                tile = grouped_pool.tile([P, C], F32, name="gated")
-            nc.vector.tensor_tensor(tile[:], y[:], gate_sb[:, e * C : (e + 1) * C], MULT)
-            return tile
-
-        def store(half):
-            nc.sync.dma_start(out=out[half * P : (half + 1) * P, :], in_=out_sb[half][:])
-
-        def scatter_gated(engine, e, half, tile):
-            if engine == "S":
-                nc.scalar.activation(places(e, half), tile[:], COPY)
-            else:
-                nc.vector.tensor_copy(places(e, half), tile[:])
-
-        a, b = LAST - 1, LAST
-        a0 = interleave(raws[a, 0], 0, P, "S", "grouped2")
-        h_last = square_and_quantise(b, last_relu(raws[a, 0]))
-        b0 = interleave(raws[b, 0], 0, P, "V", "grouped2")
-        quantise("w2", a, 0, 0, P, a0)
-        ya0 = product(a, *weights["w2", a, 0], y_psum.tile([P, C], F32, name="y0"))
-        quantise("w2", b, 0, 0, P, b0)
-        first = weights["w2", b, 0]
-        a1 = interleave(raws[a, 1], 0, P, "V", "grouped2")
-        quantise("w2", a, 0, P, P, a1)
-        ya1 = product(a, *weights["w2", a, 0], y_psum.tile([P, C], F32, name="y1"))
-        ga0 = gated(a, ya0, raws[a, 1][:, 0, :])
-        scatter_gated("S", a, 0, ga0)
-        b1 = interleave(raws[b, 1], 0, P, "V", "grouped2")
-        quantise_h(b, h_last)
-        yb0 = product(b, *first, sum_psum.tile([P, C], F32, name="bank"))
-        quantise("w2", b, 0, P, P, b1)
-        yb1 = product(b, *weights["w2", b, 0], sum_psum.tile([P, C], F32, name="bank"))
-        ga1 = gated(a, ya1, relu_pool.tile([P, C], F32, name="h_last", align_bytes=MX_ALIGN))
-        scatter_gated("S", a, 1, ga1)
-        gb0 = gated(b, yb0)
-        gb1 = gated(b, yb1)
-        scatter_gated("V", b, 0, gb0)
+        before = LAST - 1
+        rounded = {(before, 0): interleave(halves[before, 0], 0, P, "S", "grouped2")}
+        relu = last_relu(halves[before, 0])
+        h_last = square(relu, end_pool.tile([P, C * PACK], BF16, name="h_last", align_bytes=MX_ALIGN))
+        rounded[LAST, 0] = interleave(halves[LAST, 0], 0, P, "V", "grouped2")
+        w_codes = {(before, 0): half_codes(before, 0, rounded[before, 0])}
+        y = {(before, 0): second_layer(before, *w_codes[before, 0], y_psum.tile([P, C], F32, name="y0")[:])}
+        w_codes[LAST, 0] = half_codes(LAST, 0, rounded[LAST, 0])
+        rounded[before, 1] = interleave(halves[before, 1], 0, P, "V", "grouped2")
+        w_codes[before, 1] = half_codes(before, 1, rounded[before, 1])
+        y[before, 1] = second_layer(before, *w_codes[before, 1], y_psum.tile([P, C], F32, name="y1")[:])
+        results = {(before, 0): gated(before, y[before, 0], halves[before, 1][:, 0, :])}
+        nc.scalar.activation(places(before, 0), results[before, 0], COPY)
+        rounded[LAST, 1] = interleave(halves[LAST, 1], 0, P, "V", "grouped2")
+        quantise_h(LAST, h_last)
+        y[LAST, 0] = second_layer(LAST, *w_codes[LAST, 0], sum_psum.tile([P, C], F32, name="bank")[:])
+        w_codes[LAST, 1] = half_codes(LAST, 1, rounded[LAST, 1])
+        y[LAST, 1] = second_layer(LAST, *w_codes[LAST, 1], sum_psum.tile([P, C], F32, name="bank")[:])
+        behind_h = end_pool.tile([P, C], F32, name="h_last", align_bytes=MX_ALIGN)
+        results[before, 1] = gated(before, y[before, 1], behind_h[:])
+        nc.scalar.activation(places(before, 1), results[before, 1], COPY)
+        for half in range(HALVES):
+            results[LAST, half] = gated(LAST, y[LAST, half], grouped_pool.tile([P, C], F32, name="gated")[:])
+        nc.vector.tensor_copy(places(LAST, 0), results[LAST, 0])
         store(0)
-        scatter_gated("S", b, 1, gb1)
+        nc.scalar.activation(places(LAST, 1), results[LAST, 1], COPY)
         store(1)

@@ -35,6 +35,7 @@ DMA_ALIGN = 256
 X_COPIERS = ("V", "S")
 W1_COPIERS = ("S", "V")
 PAIR_COPIERS = ("V", "S")
+EARLY_COPIERS = ("S", "S")
 W2_COPIER = "S"
 
 
@@ -160,7 +161,7 @@ def tile_moe_two_mlp_relu2_kernel(tc, xT, w1, w2, gate, offs, dst, out):
             tiles = [grouped_pool.tile([P, 2 * P * PACK], BF16, name="pair", align_bytes=MX_ALIGN) for u in range(2)]
             for n, part in enumerate(parts):
                 columns = slice(n * P // len(parts), (n + 1) * P // len(parts))
-                for u, copier in enumerate(PAIR_COPIERS):
+                for u, copier in enumerate(EARLY_COPIERS if n + 1 < len(parts) else PAIR_COPIERS):
                     dest = tiles[u][:].rearrange("p (v m j) -> p m j v", v=2, j=PACK)
                     move(copier, dest[:, columns], by_pairs(part)[:, u])
             together = 1 if ("w1", e, s) == last_pass else 2

@@ -31,26 +31,21 @@ GATE_BLOCKS = E // GATE_ROWS
 LIST_ROWS = 16
 MX_ALIGN = 256
 DMA_ALIGN = 256
-
-X_COPIERS = ("V", "S")
-W1_COPIERS = ("S", "V")
-PAIR_COPIERS = ("V", "S")
-EARLY_COPIERS = ("S", "S")
-W2_COPIER = "S"
+LATE = 3
 
 
 def tile_moe_two_mlp_relu2_kernel(tc, xT, w1, w2, gate, offs, dst, out):
     nc = tc.nc
 
     loads = [("x", 0, s) for s in range(PASSES)]
-    for e in range(E):
-        loads.extend(("w1", e, s) for s in range(PASSES - 1))
-        if 0 < e < LAST:
-            loads.append(("w2", e - 1, 0))
-        loads.append(("w1", e, PASSES - 1))
-    loads.extend(("half", e, half) for half in range(HALVES) for e in (LAST - 1, LAST))
-    last_pass = ("w1", LAST, PASSES - 1)
-    dst_behind = ("w2", 0, 0)
+    for e in range(LAST):
+        loads.extend((("w1", e, 0), ("w1", e, 1)))
+        if e > 0:
+            loads.append(("w2", e - 1, 0) if e - 1 < LATE else ("half", e - 1, 0))
+        loads.append(("w1", e, 2))
+    loads.extend((("w1", LAST, 0), ("w1", LAST, 1), ("left", LAST, 2), ("right", LAST, 2)))
+    loads.extend((("half", 4, 0), ("half", 3, 1), ("half", LAST, 0), ("half", 4, 1), ("half", LAST, 1)))
+    streamed = loads.index(("left", LAST, 2))
 
     with ExitStack() as ctx:
         keep = ctx.enter_context(tc.tile_pool(name="keep", bufs=1))
@@ -59,8 +54,7 @@ def tile_moe_two_mlp_relu2_kernel(tc, xT, w1, w2, gate, offs, dst, out):
         raw2_pool = ctx.enter_context(tc.tile_pool(name="raw2", bufs=2))
         grouped_pool = ctx.enter_context(tc.tile_pool(name="grouped", bufs=4))
         code_pool = ctx.enter_context(tc.tile_pool(name="codes", bufs=PASSES + 1))
-        small_pool = ctx.enter_context(tc.tile_pool(name="small", bufs=3))
-        end_pool = ctx.enter_context(tc.tile_pool(name="relu", bufs=1))
+        small_pool = ctx.enter_context(tc.tile_pool(name="small", bufs=2))
         sum_psum = ctx.enter_context(tc.psum_pool(name="sum_psum", bufs=2))
         last_psum = ctx.enter_context(tc.psum_pool(name="last_psum", bufs=1))
         y_psum = ctx.enter_context(tc.psum_pool(name="y_psum", bufs=1))
@@ -96,39 +90,38 @@ def tile_moe_two_mlp_relu2_kernel(tc, xT, w1, w2, gate, offs, dst, out):
                 width = GATE_BLOCKS * C
                 nc.scalar.copy(out=gate_sb[:, r * width : (r + 1) * width], in_=spread[:].rearrange("p b c -> p (b c)"))
 
-        raws, halves, weights, hidden, sums = {}, {}, {}, {}, {}
+        raws, weights, hidden, sums = {}, {}, {}, {}
 
-        def load(i):
-            tensor, e, s = loads[i]
+        def load(item):
+            tensor, e, s = item
             if tensor == "x":
                 raw = rawx_pool.tile([P, PACK, T], F32, name="rawx", align_bytes=DMA_ALIGN)
                 src = xT[s * PASS : (s + 1) * PASS, :]
             elif tensor == "w1":
                 raw = raw_pool.tile([P, PACK, H], F32, name="raw", align_bytes=DMA_ALIGN)
                 src = w1[e, s * PASS : (s + 1) * PASS, :]
+            elif tensor in ("left", "right"):
+                raw = raw_pool.tile([P, PACK, H // 2], F32, name="raw", align_bytes=DMA_ALIGN)
+                first = 0 if tensor == "left" else H // 2
+                src = w1[e, s * PASS : (s + 1) * PASS, first : first + H // 2]
+            elif tensor == "half" and e < LAST - 1 and s == 0:
+                raw = raw2_pool.tile([P, PACK, P], F32, name="raw2", align_bytes=DMA_ALIGN)
+                src = w2[e, :, 0:P]
             elif tensor == "half":
                 raw = keep.tile([P, PACK, P], F32, name=f"half{e}{s}", align_bytes=DMA_ALIGN)
                 src = w2[e, :, s * P : (s + 1) * P]
             else:
                 raw = raw2_pool.tile([P, PACK, N], F32, name="raw2", align_bytes=DMA_ALIGN)
                 src = w2[e]
-            src = src.rearrange("(p j) c -> p j c", j=PACK)
-            if loads[i] == last_pass:
-                right = raw_pool.tile([P, PACK, H // 2], F32, name="raw", align_bytes=DMA_ALIGN)
-                left = raw[:].rearrange("p j c -> p (j c)")[:, 0 : PACK * H // 2].rearrange("p (j c) -> p j c", j=PACK)
-                nc.sync.dma_start(out=left, in_=src[:, :, 0 : H // 2])
-                nc.sync.dma_start(out=right[:], in_=src[:, :, H // 2 : H])
-                raws[i] = (left, right[:])
-                return
-            nc.sync.dma_start(out=raw[:], in_=src)
-            raws[i] = raw[:]
-            if i == 0:
+            nc.sync.dma_start(out=raw[:], in_=src.rearrange("(p j) c -> p j c", j=PACK))
+            raws[item] = raw[:]
+            if item == ("x", 0, 0):
                 nc.sync.dma_start(offs_sb[:], offs)
-            if i == 1:
+            if item == ("x", 0, 1):
                 nc.sync.dma_start(
                     out=gate_rows[0:GATE_ROWS, :], in_=gate[0:1, :].rearrange("o (r c) -> (o r) c", r=GATE_ROWS)
                 )
-            if loads[i] == dst_behind:
+            if item == ("w2", 0, 0):
                 nc.sync.dma_start(dst_sb[:], dst)
 
         def move(copier, dest, src):
@@ -137,62 +130,82 @@ def tile_moe_two_mlp_relu2_kernel(tc, xT, w1, w2, gate, offs, dst, out):
             else:
                 nc.vector.tensor_copy(out=dest, in_=src)
 
-        def interleave(raw, first, width, copier, tag):
-            tile = grouped_pool.tile([P, width * PACK], BF16, name=tag, align_bytes=MX_ALIGN)
+        def interleave(raw, first, width, copier, tile):
             src = raw[:, :, first : first + width].rearrange("p j (c i) -> p c j i", i=4)
-            move(copier, tile[:].rearrange("p (c i j) -> p c j i", i=4, j=PACK), src)
+            move(copier, tile.rearrange("p (c i j) -> p c j i", i=4, j=PACK), src)
             return tile
+
+        def rounded(width, tag, bufs=4):
+            return grouped_pool.tile([P, width * PACK], BF16, name=tag, bufs=bufs, align_bytes=MX_ALIGN)[:]
 
         def by_pairs(raw):
             return raw.rearrange("p j (m u v) -> p u m j v", u=2, v=2)
 
-        def interleave_w1(raw, copier):
-            tile = grouped_pool.tile([P, H * PACK], BF16, name="grouped", align_bytes=MX_ALIGN)
-            move(copier, tile[:].rearrange("p (u v m j) -> p u m j v", u=2, v=2, j=PACK), by_pairs(raw))
-            return tile
-
-        def shared_pass(e, s, parts):
+        def w1_codes(e, s):
             codes = code_pool.tile([P, H], U32, name="codes_w1", align_bytes=MX_ALIGN)[:, :]
             scales = code_pool.tile([P, H], U8, name="scales_w1", align_bytes=MX_ALIGN)[:, :]
-            weights["w1", e, s] = (codes, scales)
-            if (e, s) == (LAST, 0):
-                for group in range(PACK):
-                    sums[group] = last_psum.tile([P, C], F32, name=f"last{group}")
-            tiles = [grouped_pool.tile([P, 2 * P * PACK], BF16, name="pair", align_bytes=MX_ALIGN) for u in range(2)]
-            for n, part in enumerate(parts):
-                columns = slice(n * P // len(parts), (n + 1) * P // len(parts))
-                for u, copier in enumerate(EARLY_COPIERS if n + 1 < len(parts) else PAIR_COPIERS):
-                    dest = tiles[u][:].rearrange("p (v m j) -> p m j v", v=2, j=PACK)
-                    move(copier, dest[:, columns], by_pairs(part)[:, u])
-            together = 1 if ("w1", e, s) == last_pass else 2
-            for first in range(0, PACK, together):
-                chans = slice(first * P, (first + together) * P)
-                values = tiles[first // 2][:, first % 2 * PASS : (first % 2 + together) * PASS]
-                nc.vector.quantize_mx(out=codes[:, chans].bitcast(FP8X4), scales=scales[:, chans], in_=values)
-                for group in range(first, first + together):
+            weights[e, s] = (codes, scales)
+            return codes, scales
+
+        def quantise(codes, scales, values):
+            nc.vector.quantize_mx(out=codes.bitcast(FP8X4), scales=scales, in_=values)
+
+        def multiply(into, stationary, moving, start, stop):
+            nc.tensor.matmul_mx(
+                out=into,
+                lhsT=stationary[0].bitcast(FP8X4),
+                lhsT_scale=stationary[1],
+                rhs=moving[0].bitcast(FP8X4),
+                rhs_scale=moving[1],
+                start=start,
+                stop=stop,
+            )
+
+        def first_layer(e, group, s, into, start, stop):
+            codes, scales = weights[e, s]
+            chans = slice(group * P, (group + 1) * P)
+            slots = slice(e * C, (e + 1) * C)
+            tokens = (slot_codes[s][:, slots], slot_scales[4 * s : P, slots])
+            multiply(into, (codes[:, chans], scales[:, chans]), tokens, start, stop)
+
+        def whole_pass(e, s, copier):
+            tile = rounded(H, "grouped")
+            move(copier, tile.rearrange("p (u v m j) -> p u m j v", u=2, v=2, j=PACK), by_pairs(raws["w1", e, s]))
+            quantise(*w1_codes(e, s), tile)
+            if s == 0:
+                sums["bank", e] = sum_psum.tile([P, PACK, C], F32, name="bank")
+            for group in range(PACK):
+                first_layer(e, group, s, sums["bank", e][:, group, :], (s, group) == (0, 0), False)
+
+        def copy_pair(tile, raw, u, columns, copier):
+            move(copier, tile.rearrange("p (v m j) -> p m j v", v=2, j=PACK)[:, columns], by_pairs(raw)[:, u])
+
+        def shared_pass(e, s):
+            codes, scales = w1_codes(e, s)
+            tiles = [rounded(2 * P, "pair") for u in range(2)]
+            for u, copier in enumerate("VS"):
+                copy_pair(tiles[u], raws["w1", e, s], u, slice(0, P), copier)
+            for u in range(2):
+                chans = slice(2 * u * P, (2 * u + 2) * P)
+                quantise(codes[:, chans], scales[:, chans], tiles[u])
+                for group in (2 * u, 2 * u + 1):
                     if e < LAST:
                         first_layer(e, group, s, sums["bank", e][:, group, :], False, group == PACK - 1)
                     elif s == 1:
+                        sums[group] = last_psum.tile([P, C], F32, name=f"last{group}")
                         first_layer(e, group, 1, sums[group][:], True, False)
                         first_layer(e, group, 0, sums[group][:], False, False)
-                    elif s == PASSES - 1:
-                        first_layer(e, group, s, sums[group][:], False, True)
-
-        def quantise(tensor, e, s, first, width, tile):
-            if tensor == "x":
-                codes = x_codes[s][:, first : first + width]
-                scales = x_scales[4 * s : P, first : first + width]
-            else:
-                codes = code_pool.tile([P, width], U32, name="codes_" + tensor, align_bytes=MX_ALIGN)[:, :]
-                scales = code_pool.tile([P, width], U8, name="scales_" + tensor, align_bytes=MX_ALIGN)[:, :]
-                weights[tensor, e, s] = (codes, scales)
-            nc.vector.quantize_mx(out=codes.bitcast(FP8X4), scales=scales, in_=tile[:])
 
         def gather(slots, table, first, end):
             listed = offs_sb[:, first // LIST_ROWS : end // LIST_ROWS]
             nc.vector.tensor_copy(slots[:, first:end], table[:].indirect(listed))
 
-        def gather_pass(s):
+        def tokens_pass(s):
+            raw = raws["x", 0, s]
+            tiles = [interleave(raw, n * WIDTH, WIDTH, copier, rounded(WIDTH, "grouped")) for n, copier in enumerate("VS")]
+            for n, tile in enumerate(tiles):
+                columns = slice(n * WIDTH, (n + 1) * WIDTH)
+                quantise(x_codes[s][:, columns], x_scales[4 * s : P, columns], tile)
             if s < PASSES - 1:
                 gather(slot_codes[s], x_codes[s], 0, SLOTS)
                 return
@@ -200,151 +213,127 @@ def tile_moe_two_mlp_relu2_kernel(tc, xT, w1, w2, gate, offs, dst, out):
                 gather(slot_codes[s], x_codes[s], first, end)
                 gather(slot_scales, x_scales, first, end)
 
-        def first_layer(e, group, s, into, start, stop):
-            codes, scales = weights["w1", e, s]
-            chans = slice(group * P, (group + 1) * P)
-            slots = slice(e * C, (e + 1) * C)
-            nc.tensor.matmul_mx(
-                out=into,
-                lhsT=codes[:, chans].bitcast(FP8X4),
-                lhsT_scale=scales[:, chans],
-                rhs=slot_codes[s][:, slots].bitcast(FP8X4),
-                rhs_scale=slot_scales[4 * s : P, slots],
-                start=start,
-                stop=stop,
-            )
-
-        def first_layer_pass(e, s):
-            if s == 0:
-                sums["bank", e] = sum_psum.tile([P, PACK, C], F32, name="bank")
-            for group in range(PACK):
-                first_layer(e, group, s, sums["bank", e][:, group, :], (s, group) == (0, 0), False)
-
-        def bank_relu(e, relu):
-            nc.scalar.activation(relu, sums["bank", e][:].rearrange("p t c -> p c t"), RELU)
-            return relu
-
-        def last_relu(relu):
-            for group in range(PACK):
-                nc.scalar.activation(relu[:, group, :], sums[group][:], RELU)
-            return relu.rearrange("p t c -> p c t")
-
-        def square(relu, tile):
-            nc.scalar.activation(tile[:].rearrange("p (c t) -> p c t", t=PACK), relu, SQUARE)
-            return tile
-
         def quantise_h(e, tile):
-            codes = small_pool.tile([P, C], U32, name="h_codes", align_bytes=MX_ALIGN)
-            scales = small_pool.tile([P, C], U8, name="h_scales", align_bytes=MX_ALIGN)
-            nc.vector.quantize_mx(out=codes[:].bitcast(FP8X4), scales=scales[:], in_=tile[:])
-            hidden[e] = (codes, scales)
+            codes = keep.tile([P, C], U32, name=f"h_codes{e}", align_bytes=MX_ALIGN)
+            scales = keep.tile([P, C], U8, name=f"h_scales{e}", align_bytes=MX_ALIGN)
+            quantise(codes[:], scales[:], tile)
+            hidden[e] = (codes[:], scales[:])
 
-        def square_and_quantise(e, relu):
-            quantise_h(e, square(relu, small_pool.tile([P, C * PACK], BF16, name="h", align_bytes=MX_ALIGN)))
+        def square(relu):
+            tile = small_pool.tile([P, C * PACK], BF16, name="h", align_bytes=MX_ALIGN)
+            nc.scalar.activation(tile[:].rearrange("p (c t) -> p c t", t=PACK), relu, SQUARE)
+            return tile[:]
 
-        def second_layer(e, codes, scales, into):
-            h_codes, h_scales = hidden[e]
-            nc.tensor.matmul_mx(
-                out=into,
-                lhsT=codes.bitcast(FP8X4),
-                lhsT_scale=scales,
-                rhs=h_codes[:].bitcast(FP8X4),
-                rhs_scale=h_scales[:],
-                start=True,
-                stop=True,
-            )
-            return into
+        def hidden_codes(e, relu):
+            nc.scalar.activation(relu, sums["bank", e][:].rearrange("p t c -> p c t"), RELU)
+            quantise_h(e, square(relu))
 
-        def products(e, raw):
-            quantise("w2", e, 0, 0, N, interleave(raw, 0, N, W2_COPIER, "grouped2"))
-            codes, scales = weights["w2", e, 0]
-            y = y_psum.tile([P, HALVES, C], F32, name="y0")
-            for half in range(HALVES):
+        def w2_codes(width, values, tag, bufs=5):
+            codes = code_pool.tile([P, width], U32, name="codes_" + tag, bufs=bufs, align_bytes=MX_ALIGN)[:, :]
+            scales = code_pool.tile([P, width], U8, name="scales_" + tag, bufs=bufs, align_bytes=MX_ALIGN)[:, :]
+            quantise(codes, scales, values)
+            return codes, scales
+
+        def products(e, raw, halves):
+            codes, scales = w2_codes(halves * P, interleave(raw, 0, halves * P, "S", rounded(halves * P, "grouped2", 2)), "w2", 2)
+            y = y_psum.tile([P, halves, C], F32, name="y0")
+            for half in range(halves):
                 chans = slice(half * P, (half + 1) * P)
-                second_layer(e, codes[:, chans], scales[:, chans], y[:, half, :])
+                multiply(y[:, half, :], (codes[:, chans], scales[:, chans]), hidden[e], True, True)
             return y
 
-        def places(e, half):
-            return out_sb[half][:].indirect(dst_sb[:, e * C // LIST_ROWS : (e + 1) * C // LIST_ROWS])
+        def places(half, first, end):
+            return out_sb[half][:].indirect(dst_sb[:, first * C // LIST_ROWS : end * C // LIST_ROWS])
 
-        def gates(e):
-            return gate_sb[:, e * C : (e + 1) * C]
+        def gates(first, end):
+            return gate_sb[:, first * C : end * C]
 
-        def scatter_times_gate(e, y, y_sb):
+        def scatter_times_gate(e, y, y_sb, halves):
             nc.scalar.copy(out=y_sb, in_=y[:])
-            for half in range(HALVES):
-                nc.vector.tensor_tensor(places(e, half), y_sb[:, half, :], gates(e), MULT)
-
-        def half_codes(e, half, tile):
-            quantise("w2", e, half, 0, P, tile)
-            return weights["w2", e, half]
-
-        def gated(e, y, into):
-            nc.vector.tensor_tensor(into, y, gates(e), MULT)
-            return into
+            for half in range(halves):
+                nc.vector.tensor_tensor(places(half, e, e + 1), y_sb[:, half, :], gates(e, e + 1), MULT)
 
         def store(half):
             nc.sync.dma_start(out=out[half * P : (half + 1) * P, :], in_=out_sb[half][:])
 
-        for i in range(AHEAD):
-            load(i)
-        for i, (tensor, e, s) in enumerate(loads):
-            if i + AHEAD < len(loads):
-                load(i + AHEAD)
-            raw = raws.pop(i)
-            if (tensor, s) == ("x", 2):
-                spread_gate()
+        for item in loads[:AHEAD]:
+            load(item)
+        for i, item in enumerate(loads[:streamed]):
+            load(loads[i + AHEAD])
+            tensor, e, s = item
+            raw = raws[item]
             if tensor == "x":
-                tiles = [interleave(raw, n * WIDTH, WIDTH, copier, "grouped") for n, copier in enumerate(X_COPIERS)]
-                for n, tile in enumerate(tiles):
-                    quantise(tensor, e, s, n * WIDTH, WIDTH, tile)
-                gather_pass(s)
+                if s == 2:
+                    spread_gate()
+                tokens_pass(s)
             elif tensor == "w1":
-                if loads[i] == last_pass:
-                    shared_pass(e, s, raw)
-                elif e == LAST or s == PASSES - 1:
-                    shared_pass(e, s, (raw,))
+                if e == LAST or s == PASSES - 1:
+                    shared_pass(e, s)
                 else:
-                    quantise(tensor, e, s, 0, H, interleave_w1(raw, W1_COPIERS[s]))
-                    first_layer_pass(e, s)
+                    whole_pass(e, s, "SV"[s])
                 if s == 0 and 0 < e < LAST:
-                    spent = raw[:, 0, :].rearrange("p (c t) -> p c t", t=PACK)
-                    square_and_quantise(e - 1, bank_relu(e - 1, spent))
-                if s == PASSES - 1 and 0 < e < LAST:
-                    spent = raw[:, 0, 0 : HALVES * C].rearrange("p (n c) -> p n c", c=C)
-                    scatter_times_gate(e - 1, products_waiting, spent)
+                    hidden_codes(e - 1, raw[:, 0, :].rearrange("p (c t) -> p c t", t=PACK))
+                if s == PASSES - 1 and e > 0:
+                    halves = waiting[1]
+                    spent = raw[:, 0, 0 : halves * C].rearrange("p (n c) -> p n c", c=C)
+                    scatter_times_gate(e - 1, waiting[0], spent, halves)
                 if (e, s) == (LAST - 1, PASSES - 1):
-                    relu = end_pool.tile([P, C, PACK], F32, name="relu", align_bytes=MX_ALIGN)
-                    square_and_quantise(e, bank_relu(e, relu[:]))
-            elif tensor == "w2":
-                products_waiting = products(e, raw)
+                    relu = keep.tile([P, C, PACK], F32, name="relu", align_bytes=MX_ALIGN)
+                    hidden_codes(e, relu[:])
             else:
-                halves[e, s] = raw
+                halves = HALVES if tensor == "w2" else 1
+                waiting = (products(e, raw, halves), halves)
+        for item in loads[streamed + AHEAD :]:
+            load(item)
 
-        before = LAST - 1
-        rounded = {(before, 0): interleave(halves[before, 0], 0, P, "S", "grouped2")}
-        relu = last_relu(halves[before, 0])
-        h_last = square(relu, end_pool.tile([P, C * PACK], BF16, name="h_last", align_bytes=MX_ALIGN))
-        rounded[LAST, 0] = interleave(halves[LAST, 0], 0, P, "V", "grouped2")
-        w_codes = {(before, 0): half_codes(before, 0, rounded[before, 0])}
-        y = {(before, 0): second_layer(before, *w_codes[before, 0], y_psum.tile([P, C], F32, name="y0")[:])}
-        w_codes[LAST, 0] = half_codes(LAST, 0, rounded[LAST, 0])
-        rounded[before, 1] = interleave(halves[before, 1], 0, P, "V", "grouped2")
-        w_codes[before, 1] = half_codes(before, 1, rounded[before, 1])
-        y[before, 1] = second_layer(before, *w_codes[before, 1], y_psum.tile([P, C], F32, name="y1")[:])
-        results = {(before, 0): gated(before, y[before, 0], halves[before, 1][:, 0, :])}
-        nc.scalar.activation(places(before, 0), results[before, 0], COPY)
-        rounded[LAST, 1] = interleave(halves[LAST, 1], 0, P, "V", "grouped2")
+        codes, scales = w1_codes(LAST, 2)
+        pairs = [rounded(2 * P, "pair") for u in range(2)]
+        for n, side in enumerate(("left", "right")):
+            for u, copier in enumerate(("SS", "VS")[n]):
+                copy_pair(pairs[u], raws[side, LAST, 2], u, slice(n * P // 2, (n + 1) * P // 2), copier)
+        for group in range(PACK):
+            chans = slice(group * P, (group + 1) * P)
+            quantise(codes[:, chans], scales[:, chans], pairs[group // 2][:, group % 2 * PASS : (group % 2 + 1) * PASS])
+            first_layer(LAST, group, 2, sums[group][:], False, True)
+
+        def copy_half(e, half, copier):
+            tile = keep.tile([P, PASS], BF16, name=f"rounded{e}{half}", align_bytes=MX_ALIGN)
+            return interleave(raws["half", e, half], 0, P, copier, tile[:])
+
+        def gated(y, first, end, name):
+            tile = keep.tile([P, (end - first) * C], F32, name=name)
+            nc.vector.tensor_tensor(tile[:], y, gates(first, end), MULT)
+            return tile[:]
+
+        y40 = y_psum.tile([P, C], F32, name="y0")
+        y31 = y_psum.tile([P, C], F32, name="y1")
+        y41 = sum_psum.tile([P, C], F32, name="bank")
+        y50 = sum_psum.tile([P, C], F32, name="bank")
+        values = {(4, 0): copy_half(4, 0, "S"), (3, 1): copy_half(3, 1, "V")}
+        multiply(y40[:], w2_codes(P, values[4, 0], "half"), hidden[4], True, True)
+        relu = keep.tile([P, PACK, C], F32, name="last_relu", align_bytes=MX_ALIGN)
+        for group in range(PACK):
+            nc.scalar.activation(relu[:, group, :], sums[group][:], RELU)
+        values[5, 0] = copy_half(LAST, 0, "V")
+        multiply(y31[:], w2_codes(P, values[3, 1], "half"), hidden[3], True, True)
+        values[4, 1] = copy_half(4, 1, "V")
+        y40_sb = gated(y40[:], 4, 5, "y40_sb")
+        last_codes = w2_codes(P, values[5, 0], "half")
+        h_last = square(relu[:].rearrange("p t c -> p c t"))
+        nc.scalar.activation(places(0, 4, 5), y40_sb, COPY)
+        values[5, 1] = copy_half(LAST, 1, "V")
+        y31_sb = gated(y31[:], 3, 4, "y31_sb")
         quantise_h(LAST, h_last)
-        y[LAST, 0] = second_layer(LAST, *w_codes[LAST, 0], sum_psum.tile([P, C], F32, name="bank")[:])
-        w_codes[LAST, 1] = half_codes(LAST, 1, rounded[LAST, 1])
-        y[LAST, 1] = second_layer(LAST, *w_codes[LAST, 1], sum_psum.tile([P, C], F32, name="bank")[:])
-        behind_h = end_pool.tile([P, C], F32, name="h_last", align_bytes=MX_ALIGN)
-        results[before, 1] = gated(before, y[before, 1], behind_h[:])
-        nc.scalar.activation(places(before, 1), results[before, 1], COPY)
-        for half in range(HALVES):
-            results[LAST, half] = gated(LAST, y[LAST, half], grouped_pool.tile([P, C], F32, name="gated")[:])
-        nc.vector.tensor_copy(places(LAST, 0), results[LAST, 0])
+        multiply(y50[:], last_codes, hidden[LAST], True, True)
+        nc.scalar.activation(places(1, 3, 4), y31_sb, COPY)
+        multiply(y41[:], w2_codes(P, values[4, 1], "half"), hidden[4], True, True)
+        y51 = y_psum.tile([P, C], F32, name="y0")
+        multiply(y51[:], w2_codes(P, values[5, 1], "half"), hidden[5], True, True)
+        y50_sb = gated(y50[:], LAST, E, "y50_sb")
+        y41_sb = gated(y41[:], 4, 5, "y41_sb")
+        y51_sb = gated(y51[:], LAST, E, "y51_sb")
+        nc.scalar.activation(places(0, LAST, E), y50_sb, COPY)
         store(0)
-        nc.scalar.activation(places(LAST, 1), results[LAST, 1], COPY)
+        nc.vector.tensor_copy(places(1, 4, 5), y41_sb)
+        nc.scalar.activation(places(1, LAST, E), y51_sb, COPY)
         store(1)

@@ -43,7 +43,7 @@ def tile_moe_two_mlp_relu2_kernel(tc, xT, w1, w2, gate, offs, dst, out):
         if e > 0:
             loads.append(("w2", e - 1, 0) if e - 1 < LATE else ("half", e - 1, 0))
         loads.append(("w1", e, 2))
-    loads.extend((("w1", LAST, 0), ("w1", LAST, 1), ("left", LAST, 2), ("right", LAST, 2)))
+    loads.extend((("left", LAST, 0), ("right", LAST, 0), ("w1", LAST, 1), ("left", LAST, 2), ("right", LAST, 2)))
     loads.extend((("half", 4, 0), ("half", 3, 1), ("half", LAST, 0), ("half", 4, 1), ("half", LAST, 1)))
     streamed = loads.index(("left", LAST, 2))
 
@@ -184,7 +184,11 @@ def tile_moe_two_mlp_relu2_kernel(tc, xT, w1, w2, gate, offs, dst, out):
             codes, scales = w1_codes(e, s)
             tiles = [rounded(2 * P, "pair") for u in range(2)]
             for u, copier in enumerate("VS"):
-                copy_pair(tiles[u], raws["w1", e, s], u, slice(0, P), copier)
+                if (e, s) == (LAST, 0):
+                    copy_pair(tiles[u], raws["left", e, s], u, slice(0, P // 2), "S")
+                    copy_pair(tiles[u], raws["right", e, s], u, slice(P // 2, P), "V")
+                else:
+                    copy_pair(tiles[u], raws["w1", e, s], u, slice(0, P), copier)
             for u in range(2):
                 chans = slice(2 * u * P, (2 * u + 2) * P)
                 quantise(codes[:, chans], scales[:, chans], tiles[u])
@@ -280,7 +284,9 @@ def tile_moe_two_mlp_relu2_kernel(tc, xT, w1, w2, gate, offs, dst, out):
                 if (e, s) == (LAST - 1, PASSES - 1):
                     relu = keep.tile([P, C, PACK], F32, name="relu", align_bytes=MX_ALIGN)
                     hidden_codes(e, relu[:])
-            else:
+            elif tensor == "right":
+                shared_pass(e, s)
+            elif tensor != "left":
                 halves = HALVES if tensor == "w2" else 1
                 waiting = (products(e, raw, halves), halves)
         for item in loads[streamed + AHEAD :]:
@@ -289,12 +295,14 @@ def tile_moe_two_mlp_relu2_kernel(tc, xT, w1, w2, gate, offs, dst, out):
         codes, scales = w1_codes(LAST, 2)
         pairs = [rounded(2 * P, "pair") for u in range(2)]
         for n, side in enumerate(("left", "right")):
-            for u, copier in enumerate(("SS", "VS")[n]):
+            for u, copier in enumerate("VS"):
                 copy_pair(pairs[u], raws[side, LAST, 2], u, slice(n * P // 2, (n + 1) * P // 2), copier)
-        for group in range(PACK):
-            chans = slice(group * P, (group + 1) * P)
-            quantise(codes[:, chans], scales[:, chans], pairs[group // 2][:, group % 2 * PASS : (group % 2 + 1) * PASS])
-            first_layer(LAST, group, 2, sums[group][:], False, True)
+            for group in range(PACK):
+                chans = slice(group * P + n * P // 2, group * P + (n + 1) * P // 2)
+                at = (group % 2 * P + n * P // 2) * PACK
+                quantise(codes[:, chans], scales[:, chans], pairs[group // 2][:, at : at + PASS // 2])
+                if n == 1:
+                    first_layer(LAST, group, 2, sums[group][:], False, True)
 
         def copy_half(e, half, copier):
             tile = keep.tile([P, PASS], BF16, name=f"rounded{e}{half}", align_bytes=MX_ALIGN)

@@ -295,8 +295,13 @@ def tile_moe_two_mlp_relu2_kernel(tc, xT, w1, w2, gate, offs, dst, out):
         codes, scales = w1_codes(LAST, 2)
         pairs = [rounded(2 * P, "pair") for u in range(2)]
         for n, side in enumerate(("left", "right")):
-            for u, copier in enumerate("VS"):
-                copy_pair(pairs[u], raws[side, LAST, 2], u, slice(n * P // 2, (n + 1) * P // 2), copier)
+            raw = raws[side, LAST, 2]
+            copy_pair(pairs[0], raw, 0, slice(n * P // 2, (n + 1) * P // 2), "V")
+            if n == 0:
+                copy_pair(pairs[1], raw, 1, slice(0, P // 2), "S")
+            else:
+                copy_pair(pairs[1], raw[:, :, 0 : H // 4], 1, slice(P // 2, 3 * P // 4), "S")
+                copy_pair(pairs[1], raw[:, :, H // 4 : H // 2], 1, slice(3 * P // 4, P), "V")
             for group in range(PACK):
                 chans = slice(group * P + n * P // 2, group * P + (n + 1) * P // 2)
                 at = (group % 2 * P + n * P // 2) * PACK
@@ -304,44 +309,51 @@ def tile_moe_two_mlp_relu2_kernel(tc, xT, w1, w2, gate, offs, dst, out):
                 if n == 1:
                     first_layer(LAST, group, 2, sums[group][:], False, True)
 
-        def copy_half(e, half, copier):
-            tile = keep.tile([P, PASS], BF16, name=f"rounded{e}{half}", align_bytes=MX_ALIGN)
+        def copy_half(e, half, copier, tag):
+            tile = keep.tile([P, PASS], BF16, name=tag, align_bytes=MX_ALIGN)
             return interleave(raws["half", e, half], 0, P, copier, tile[:])
 
-        def gated(y, first, end, name):
-            tile = keep.tile([P, (end - first) * C], F32, name=name)
-            nc.vector.tensor_tensor(tile[:], y, gates(first, end), MULT)
+        def half_codes(values, tag):
+            codes = keep.tile([P, P], U32, name=tag, align_bytes=MX_ALIGN)
+            scales = code_pool.tile([P, P], U8, name="scales_half", bufs=5, align_bytes=MX_ALIGN)
+            quantise(codes[:], scales[:], values)
+            return codes[:], scales[:]
+
+        def gated(y, e, name):
+            tile = keep.tile([P, C], F32, name=name)
+            nc.vector.tensor_tensor(tile[:], y[:], gates(e, e + 1), MULT)
             return tile[:]
 
         y40 = y_psum.tile([P, C], F32, name="y0")
         y31 = y_psum.tile([P, C], F32, name="y1")
         y41 = sum_psum.tile([P, C], F32, name="bank")
         y50 = sum_psum.tile([P, C], F32, name="bank")
-        values = {(4, 0): copy_half(4, 0, "S"), (3, 1): copy_half(3, 1, "V")}
-        multiply(y40[:], w2_codes(P, values[4, 0], "half"), hidden[4], True, True)
+        values = {(4, 0): copy_half(4, 0, "S", "rounded40"), (3, 1): copy_half(3, 1, "V", "rounded31")}
+        multiply(y40[:], half_codes(values[4, 0], "codes40"), hidden[4], True, True)
         relu = keep.tile([P, PACK, C], F32, name="last_relu", align_bytes=MX_ALIGN)
         for group in range(PACK):
             nc.scalar.activation(relu[:, group, :], sums[group][:], RELU)
-        values[5, 0] = copy_half(LAST, 0, "V")
-        multiply(y31[:], w2_codes(P, values[3, 1], "half"), hidden[3], True, True)
-        values[4, 1] = copy_half(4, 1, "V")
-        y40_sb = gated(y40[:], 4, 5, "y40_sb")
-        last_codes = w2_codes(P, values[5, 0], "half")
-        h_last = square(relu[:].rearrange("p t c -> p c t"))
+        values[5, 0] = copy_half(LAST, 0, "V", "rounded50")
+        multiply(y31[:], half_codes(values[3, 1], "codes31"), hidden[3], True, True)
+        y40_sb = gated(y40, 4, "y40_sb")
+        values[4, 1] = copy_half(4, 1, "V", "codes40")
+        last_codes = half_codes(values[5, 0], "codes50")
+        h_last = keep.tile([P, C * PACK], BF16, name="h_last", align_bytes=MX_ALIGN)
+        nc.scalar.activation(h_last[:].rearrange("p (c t) -> p c t", t=PACK), relu[:].rearrange("p t c -> p c t"), SQUARE)
         nc.scalar.activation(places(0, 4, 5), y40_sb, COPY)
-        values[5, 1] = copy_half(LAST, 1, "V")
-        y31_sb = gated(y31[:], 3, 4, "y31_sb")
-        quantise_h(LAST, h_last)
+        quantise_h(LAST, h_last[:])
         multiply(y50[:], last_codes, hidden[LAST], True, True)
+        y31_sb = gated(y31, 3, "y31_sb")
         nc.scalar.activation(places(1, 3, 4), y31_sb, COPY)
-        multiply(y41[:], w2_codes(P, values[4, 1], "half"), hidden[4], True, True)
+        multiply(y41[:], half_codes(values[4, 1], "codes41"), hidden[4], True, True)
+        values[5, 1] = copy_half(LAST, 1, "V", "h_last")
+        y50_sb = gated(y50, LAST, "y50_sb")
         y51 = y_psum.tile([P, C], F32, name="y0")
-        multiply(y51[:], w2_codes(P, values[5, 1], "half"), hidden[5], True, True)
-        y50_sb = gated(y50[:], LAST, E, "y50_sb")
-        y41_sb = gated(y41[:], 4, 5, "y41_sb")
-        y51_sb = gated(y51[:], LAST, E, "y51_sb")
-        nc.scalar.activation(places(0, LAST, E), y50_sb, COPY)
+        multiply(y51[:], half_codes(values[5, 1], "codes51"), hidden[LAST], True, True)
+        y41_sb = gated(y41, 4, "y41_sb")
+        nc.scalar.activation(places(1, 4, 5), y41_sb, COPY)
+        nc.vector.tensor_copy(places(0, LAST, E), y50_sb)
         store(0)
-        nc.vector.tensor_copy(places(1, 4, 5), y41_sb)
+        y51_sb = gated(y51, LAST, "y51_sb")
         nc.scalar.activation(places(1, LAST, E), y51_sb, COPY)
         store(1)

from contextlib import ExitStack

import concourse.mybir as mybir
from concourse.masks import make_identity

K, T, E, C, H, N = 1536, 1024, 6, 128, 512, 256
FLOPS = 2 * E * C * (K * H + H * N)

F32 = mybir.dt.float32
BF16 = mybir.dt.bfloat16
U32 = mybir.dt.uint32
U16 = mybir.dt.uint16
U8 = mybir.dt.uint8
FP8X4 = mybir.dt.float8_e4m3fn_x4
RELU = mybir.ActivationFunctionType.Relu
COPY = mybir.ActivationFunctionType.Copy
SQUARE = mybir.ActivationFunctionType.Square
MULT = mybir.AluOpType.mult

P = 128
PACK = 4
PASS = P * PACK
PASSES = K // PASS
SLOTS = E * C
HALVES = N // P
LAST = E - 1
WIDTH = T // 2
AHEAD = 6
GATE_ROWS = 2
GATE_BLOCKS = E // GATE_ROWS
LIST_ROWS = 16
MX_ALIGN = 256
DMA_ALIGN = 256
LATE = 3


def tile_moe_two_mlp_relu2_kernel(tc, xT, w1, w2, gate, offs, dst, out):
    nc = tc.nc

    loads = [("x", 0, s) for s in range(PASSES)]
    for e in range(LAST):
        loads.extend((("w1", e, 0), ("w1", e, 1)))
        if e > 0:
            loads.append(("w2", e - 1, 0) if e - 1 < LATE else ("half", e - 1, 0))
        loads.append(("w1", e, 2))
    loads.extend((("left", LAST, 0), ("right", LAST, 0), ("w1", LAST, 1), ("left", LAST, 2), ("right", LAST, 2)))
    loads.extend((("half", 4, 0), ("half", 3, 1), ("half", LAST, 0), ("half", 4, 1), ("half", LAST, 1)))
    streamed = loads.index(("left", LAST, 2))

    with ExitStack() as ctx:
        keep = ctx.enter_context(tc.tile_pool(name="keep", bufs=1))
        raw_pool = ctx.enter_context(tc.tile_pool(name="raw", bufs=8))
        rawx_pool = ctx.enter_context(tc.tile_pool(name="rawx", bufs=PASSES))
        raw2_pool = ctx.enter_context(tc.tile_pool(name="raw2", bufs=2))
        grouped_pool = ctx.enter_context(tc.tile_pool(name="grouped", bufs=4))
        code_pool = ctx.enter_context(tc.tile_pool(name="codes", bufs=PASSES + 1))
        small_pool = ctx.enter_context(tc.tile_pool(name="small", bufs=2))
        sum_psum = ctx.enter_context(tc.psum_pool(name="sum_psum", bufs=2))
        last_psum = ctx.enter_context(tc.psum_pool(name="last_psum", bufs=1))
        y_psum = ctx.enter_context(tc.psum_pool(name="y_psum", bufs=1))

        offs_sb = keep.tile([P, SLOTS // LIST_ROWS], U16, name="offs_sb")
        dst_sb = keep.tile([P, SLOTS // LIST_ROWS], U16, name="dst_sb")
        gate_sb = keep.tile([P, SLOTS], F32, name="gate_sb")
        x_codes = [keep.tile([P, T], U32, name=f"x_codes{s}", align_bytes=MX_ALIGN) for s in range(PASSES)]
        x_scales = keep.tile([P, T], U8, name="x_scales", align_bytes=MX_ALIGN)
        slot_codes = [keep.tile([P, SLOTS], U32, name=f"slot_codes{s}", align_bytes=MX_ALIGN) for s in range(PASSES)]
        slot_scales = keep.tile([P, SLOTS], U8, name="slot_scales", align_bytes=MX_ALIGN)
        out_sb = [keep.tile([P, T], F32, name=f"out_sb{half}", align_bytes=DMA_ALIGN) for half in range(HALVES)]

        nc.vector.memset(x_scales[:], 0)
        for half in range(HALVES):
            nc.vector.memset(out_sb[half][:], 0.0)

        identity = keep.tile([P, P], F32, name="identity")
        make_identity(nc, identity[:])
        gate_rows = keep.tile([P, GATE_BLOCKS * C], F32, name="gate_rows")
        nc.vector.memset(gate_rows[:], 0.0)

        def spread_gate():
            turned = last_psum.tile([P, GATE_BLOCKS, C], F32, name="last0")
            for b in range(GATE_BLOCKS):
                nc.tensor.transpose(turned[:, b, :], gate_rows[:, b * C : (b + 1) * C], identity[:])
            columns = keep.tile([P, GATE_BLOCKS, GATE_ROWS], F32, name="gate_columns")
            nc.scalar.copy(out=columns[:], in_=turned[:, :, 0:GATE_ROWS])
            for r in range(GATE_ROWS):
                spread = last_psum.tile([P, GATE_BLOCKS, C], F32, name=f"last{r + 1}")
                for b in range(GATE_BLOCKS):
                    nc.tensor.transpose(spread[:, b, :], columns[:, b, r : r + 1].to_broadcast([P, C]), identity[:])
                width = GATE_BLOCKS * C
                nc.scalar.copy(out=gate_sb[:, r * width : (r + 1) * width], in_=spread[:].rearrange("p b c -> p (b c)"))

        raws, weights, hidden, sums = {}, {}, {}, {}

        def load(item):
            tensor, e, s = item
            if tensor == "x":
                raw = rawx_pool.tile([P, PACK, T], F32, name="rawx", align_bytes=DMA_ALIGN)
                src = xT[s * PASS : (s + 1) * PASS, :]
            elif tensor == "w1":
                raw = raw_pool.tile([P, PACK, H], F32, name="raw", align_bytes=DMA_ALIGN)
                src = w1[e, s * PASS : (s + 1) * PASS, :]
            elif tensor in ("left", "right"):
                raw = raw_pool.tile([P, PACK, H // 2], F32, name="raw", align_bytes=DMA_ALIGN)
                first = 0 if tensor == "left" else H // 2
                src = w1[e, s * PASS : (s + 1) * PASS, first : first + H // 2]
            elif tensor == "half" and e < LAST - 1 and s == 0:
                raw = raw2_pool.tile([P, PACK, P], F32, name="raw2", align_bytes=DMA_ALIGN)
                src = w2[e, :, 0:P]
            elif tensor == "half":
                raw = keep.tile([P, PACK, P], F32, name=f"half{e}{s}", align_bytes=DMA_ALIGN)
                src = w2[e, :, s * P : (s + 1) * P]
            else:
                raw = raw2_pool.tile([P, PACK, N], F32, name="raw2", align_bytes=DMA_ALIGN)
                src = w2[e]
            nc.sync.dma_start(out=raw[:], in_=src.rearrange("(p j) c -> p j c", j=PACK))
            raws[item] = raw[:]
            if item == ("x", 0, 0):
                nc.sync.dma_start(offs_sb[:], offs)
            if item == ("x", 0, 1):
                nc.sync.dma_start(
                    out=gate_rows[0:GATE_ROWS, :], in_=gate[0:1, :].rearrange("o (r c) -> (o r) c", r=GATE_ROWS)
                )
            if item == ("w2", 0, 0):
                nc.sync.dma_start(dst_sb[:], dst)

        def move(copier, dest, src):
            if copier == "S":
                nc.scalar.copy(out=dest, in_=src)
            else:
                nc.vector.tensor_copy(out=dest, in_=src)

        def interleave(raw, first, width, copier, tile):
            src = raw[:, :, first : first + width].rearrange("p j (c i) -> p c j i", i=4)
            move(copier, tile.rearrange("p (c i j) -> p c j i", i=4, j=PACK), src)
            return tile

        def rounded(width, tag, bufs=4):
            return grouped_pool.tile([P, width * PACK], BF16, name=tag, bufs=bufs, align_bytes=MX_ALIGN)[:]

        def by_pairs(raw):
            return raw.rearrange("p j (m u v) -> p u m j v", u=2, v=2)

        def w1_codes(e, s):
            codes = code_pool.tile([P, H], U32, name="codes_w1", align_bytes=MX_ALIGN)[:, :]
            scales = code_pool.tile([P, H], U8, name="scales_w1", align_bytes=MX_ALIGN)[:, :]
            weights[e, s] = (codes, scales)
            return codes, scales

        def quantise(codes, scales, values):
            nc.vector.quantize_mx(out=codes.bitcast(FP8X4), scales=scales, in_=values)

        def multiply(into, stationary, moving, start, stop):
            nc.tensor.matmul_mx(
                out=into,
                lhsT=stationary[0].bitcast(FP8X4),
                lhsT_scale=stationary[1],
                rhs=moving[0].bitcast(FP8X4),
                rhs_scale=moving[1],
                start=start,
                stop=stop,
            )

        def first_layer(e, group, s, into, start, stop):
            codes, scales = weights[e, s]
            chans = slice(group * P, (group + 1) * P)
            slots = slice(e * C, (e + 1) * C)
            tokens = (slot_codes[s][:, slots], slot_scales[4 * s : P, slots])
            multiply(into, (codes[:, chans], scales[:, chans]), tokens, start, stop)

        def whole_pass(e, s, copier):
            tile = rounded(H, "grouped")
            move(copier, tile.rearrange("p (u v m j) -> p u m j v", u=2, v=2, j=PACK), by_pairs(raws["w1", e, s]))
            quantise(*w1_codes(e, s), tile)
            if s == 0:
                sums["bank", e] = sum_psum.tile([P, PACK, C], F32, name="bank")
            for group in range(PACK):
                first_layer(e, group, s, sums["bank", e][:, group, :], (s, group) == (0, 0), False)

        def copy_pair(tile, raw, u, columns, copier):
            move(copier, tile.rearrange("p (v m j) -> p m j v", v=2, j=PACK)[:, columns], by_pairs(raw)[:, u])

        def shared_pass(e, s):
            codes, scales = w1_codes(e, s)
            tiles = [rounded(2 * P, "pair") for u in range(2)]
            for u, copier in enumerate("VS"):
                if (e, s) == (LAST, 0):
                    copy_pair(tiles[u], raws["left", e, s], u, slice(0, P // 2), "S")
                    copy_pair(tiles[u], raws["right", e, s], u, slice(P // 2, P), "V")
                else:
                    copy_pair(tiles[u], raws["w1", e, s], u, slice(0, P), copier)
            for u in range(2):
                chans = slice(2 * u * P, (2 * u + 2) * P)
                quantise(codes[:, chans], scales[:, chans], tiles[u])
                for group in (2 * u, 2 * u + 1):
                    if e < LAST:
                        first_layer(e, group, s, sums["bank", e][:, group, :], False, group == PACK - 1)
                    elif s == 1:
                        sums[group] = last_psum.tile([P, C], F32, name=f"last{group}")
                        first_layer(e, group, 1, sums[group][:], True, False)
                        first_layer(e, group, 0, sums[group][:], False, False)

        def gather(slots, table, first, end):
            listed = offs_sb[:, first // LIST_ROWS : end // LIST_ROWS]
            nc.vector.tensor_copy(slots[:, first:end], table[:].indirect(listed))

        def tokens_pass(s):
            raw = raws["x", 0, s]
            tiles = [interleave(raw, n * WIDTH, WIDTH, copier, rounded(WIDTH, "grouped")) for n, copier in enumerate("VS")]
            for n, tile in enumerate(tiles):
                columns = slice(n * WIDTH, (n + 1) * WIDTH)
                quantise(x_codes[s][:, columns], x_scales[4 * s : P, columns], tile)
            if s < PASSES - 1:
                gather(slot_codes[s], x_codes[s], 0, SLOTS)
                return
            for first, end in ((0, 2 * C), (2 * C, SLOTS)):
                gather(slot_codes[s], x_codes[s], first, end)
                gather(slot_scales, x_scales, first, end)

        def quantise_h(e, tile):
            codes = keep.tile([P, C], U32, name=f"h_codes{e}", align_bytes=MX_ALIGN)
            scales = keep.tile([P, C], U8, name=f"h_scales{e}", align_bytes=MX_ALIGN)
            quantise(codes[:], scales[:], tile)
            hidden[e] = (codes[:], scales[:])

        def square(relu):
            tile = small_pool.tile([P, C * PACK], BF16, name="h", align_bytes=MX_ALIGN)
            nc.scalar.activation(tile[:].rearrange("p (c t) -> p c t", t=PACK), relu, SQUARE)
            return tile[:]

        def hidden_codes(e, relu):
            nc.scalar.activation(relu, sums["bank", e][:].rearrange("p t c -> p c t"), RELU)
            quantise_h(e, square(relu))

        def w2_codes(width, values, tag, bufs=5):
            codes = code_pool.tile([P, width], U32, name="codes_" + tag, bufs=bufs, align_bytes=MX_ALIGN)[:, :]
            scales = code_pool.tile([P, width], U8, name="scales_" + tag, bufs=bufs, align_bytes=MX_ALIGN)[:, :]
            quantise(codes, scales, values)
            return codes, scales

        def products(e, raw, halves):
            codes, scales = w2_codes(halves * P, interleave(raw, 0, halves * P, "S", rounded(halves * P, "grouped2", 2)), "w2", 2)
            y = y_psum.tile([P, halves, C], F32, name="y0")
            for half in range(halves):
                chans = slice(half * P, (half + 1) * P)
                multiply(y[:, half, :], (codes[:, chans], scales[:, chans]), hidden[e], True, True)
            return y

        def places(half, first, end):
            return out_sb[half][:].indirect(dst_sb[:, first * C // LIST_ROWS : end * C // LIST_ROWS])

        def gates(first, end):
            return gate_sb[:, first * C : end * C]

        def scatter_times_gate(e, y, y_sb, halves):
            nc.scalar.copy(out=y_sb, in_=y[:])
            for half in range(halves):
                nc.vector.tensor_tensor(places(half, e, e + 1), y_sb[:, half, :], gates(e, e + 1), MULT)

        def store(half):
            nc.sync.dma_start(out=out[half * P : (half + 1) * P, :], in_=out_sb[half][:])

        for item in loads[:AHEAD]:
            load(item)
        for i, item in enumerate(loads[:streamed]):
            load(loads[i + AHEAD])
            tensor, e, s = item
            raw = raws[item]
            if tensor == "x":
                if s == 2:
                    spread_gate()
                tokens_pass(s)
            elif tensor == "w1":
                if e == LAST or s == PASSES - 1:
                    shared_pass(e, s)
                else:
                    whole_pass(e, s, "SV"[s])
                if s == 0 and 0 < e < LAST:
                    hidden_codes(e - 1, raw[:, 0, :].rearrange("p (c t) -> p c t", t=PACK))
                if s == PASSES - 1 and e > 0:
                    halves = waiting[1]
                    spent = raw[:, 0, 0 : halves * C].rearrange("p (n c) -> p n c", c=C)
                    scatter_times_gate(e - 1, waiting[0], spent, halves)
                if (e, s) == (LAST - 1, PASSES - 1):
                    relu = keep.tile([P, C, PACK], F32, name="relu", align_bytes=MX_ALIGN)
                    hidden_codes(e, relu[:])
            elif tensor == "right":
                shared_pass(e, s)
            elif tensor != "left":
                halves = HALVES if tensor == "w2" else 1
                waiting = (products(e, raw, halves), halves)
        for item in loads[streamed + AHEAD :]:
            load(item)

        codes, scales = w1_codes(LAST, 2)
        pairs = [rounded(2 * P, "pair") for u in range(2)]
        for n, side in enumerate(("left", "right")):
            raw = raws[side, LAST, 2]
            copy_pair(pairs[0], raw, 0, slice(n * P // 2, (n + 1) * P // 2), "V")
            if n == 0:
                copy_pair(pairs[1], raw, 1, slice(0, P // 2), "S")
            else:
                copy_pair(pairs[1], raw[:, :, 0 : H // 4], 1, slice(P // 2, 3 * P // 4), "S")
                copy_pair(pairs[1], raw[:, :, H // 4 : H // 2], 1, slice(3 * P // 4, P), "V")
            for group in range(PACK):
                chans = slice(group * P + n * P // 2, group * P + (n + 1) * P // 2)
                at = (group % 2 * P + n * P // 2) * PACK
                quantise(codes[:, chans], scales[:, chans], pairs[group // 2][:, at : at + PASS // 2])
                if n == 1:
                    first_layer(LAST, group, 2, sums[group][:], False, True)

        def copy_half(e, half, copier, tag):
            tile = keep.tile([P, PASS], BF16, name=tag, align_bytes=MX_ALIGN)
            return interleave(raws["half", e, half], 0, P, copier, tile[:])

        def half_codes(values, tag):
            codes = keep.tile([P, P], U32, name=tag, align_bytes=MX_ALIGN)
            scales = code_pool.tile([P, P], U8, name="scales_half", bufs=5, align_bytes=MX_ALIGN)
            quantise(codes[:], scales[:], values)
            return codes[:], scales[:]

        def gated(y, e, name):
            tile = keep.tile([P, C], F32, name=name)
            nc.vector.tensor_tensor(tile[:], y[:], gates(e, e + 1), MULT)
            return tile[:]

        y40 = y_psum.tile([P, C], F32, name="y0")
        y31 = y_psum.tile([P, C], F32, name="y1")
        y41 = sum_psum.tile([P, C], F32, name="bank")
        y50 = sum_psum.tile([P, C], F32, name="bank")
        values = {(4, 0): copy_half(4, 0, "S", "rounded40"), (3, 1): copy_half(3, 1, "V", "rounded31")}
        multiply(y40[:], half_codes(values[4, 0], "codes40"), hidden[4], True, True)
        relu = keep.tile([P, PACK, C], F32, name="last_relu", align_bytes=MX_ALIGN)
        for group in range(PACK):
            nc.scalar.activation(relu[:, group, :], sums[group][:], RELU)
        values[5, 0] = copy_half(LAST, 0, "V", "rounded50")
        multiply(y31[:], half_codes(values[3, 1], "codes31"), hidden[3], True, True)
        y40_sb = gated(y40, 4, "y40_sb")
        values[4, 1] = copy_half(4, 1, "V", "codes40")
        last_codes = half_codes(values[5, 0], "codes50")
        h_last = keep.tile([P, C * PACK], BF16, name="h_last", align_bytes=MX_ALIGN)
        nc.scalar.activation(h_last[:].rearrange("p (c t) -> p c t", t=PACK), relu[:].rearrange("p t c -> p c t"), SQUARE)
        nc.scalar.activation(places(0, 4, 5), y40_sb, COPY)
        quantise_h(LAST, h_last[:])
        multiply(y50[:], last_codes, hidden[LAST], True, True)
        y31_sb = gated(y31, 3, "y31_sb")
        nc.scalar.activation(places(1, 3, 4), y31_sb, COPY)
        multiply(y41[:], half_codes(values[4, 1], "codes41"), hidden[4], True, True)
        values[5, 1] = copy_half(LAST, 1, "V", "h_last")
        y50_sb = gated(y50, LAST, "y50_sb")
        y51 = y_psum.tile([P, C], F32, name="y0")
        multiply(y51[:], half_codes(values[5, 1], "codes51"), hidden[LAST], True, True)
        y41_sb = gated(y41, 4, "y41_sb")
        nc.scalar.activation(places(1, 4, 5), y41_sb, COPY)
        nc.vector.tensor_copy(places(0, LAST, E), y50_sb)
        store(0)
        y51_sb = gated(y51, LAST, "y51_sb")
        nc.scalar.activation(places(1, LAST, E), y51_sb, COPY)
        store(1)
